import numpy as np
import ml_dtypes


def mxq(x, axis, fmt="e4m3"):
    dtype, down = {"e4m3": (ml_dtypes.float8_e4m3fn, 7), "e5m2": (ml_dtypes.float8_e5m2, 14)}[fmt]
    v = np.moveaxis(np.asarray(x, np.float32).astype(ml_dtypes.bfloat16).astype(np.float64), axis, -1)
    blocks = v.reshape(v.shape[:-1] + (-1, 32))
    amax = np.abs(blocks).max(-1, keepdims=True)
    byte = np.maximum(np.where(amax > 0, np.frexp(amax)[1] - 1 + 127, 0) - down, 1)
    scale = np.exp2(byte - 127.0)
    codes = (blocks / scale).astype(np.float32).astype(dtype).astype(np.float64)
    return np.moveaxis((codes * scale).reshape(v.shape), -1, axis)


WIDE = False


def mx_kscale(k):
    if not WIDE:
        return np.ones(k)
    levels = np.array([10, -10, 5, -5, 0])
    if k % 512:
        return np.exp2(np.random.permutation(np.resize(levels, k // 32))).repeat(32)
    a = np.empty((k // 512, 16))
    for p in range(k // 512):
        a[p, :8] = np.random.permutation(np.resize(levels, 8))
        for g in range(8):
            far = levels[np.abs(levels - a[p, g]) >= 10]
            a[p, g + 8] = far[np.random.randint(len(far))]
    return np.exp2(a.ravel()).repeat(32)


def f64(x):
    return np.asarray(x).astype(np.float64)


def striped(idx):
    return np.tile(np.asarray(idx).reshape(-1, 16).T, (8, 1)).astype(np.uint16)


def unstriped(offs):
    return offs[:16].T.reshape(-1).astype(np.int64)


E2M1 = np.array([0.0, 0.5, 1.0, 1.5, 2.0, 3.0, 4.0, 6.0, -0.0, -0.5, -1.0, -1.5, -2.0, -3.0, -4.0, -6.0])


def pack_weight(w, fmt):
    k, n = w.shape
    w = f64(np.asarray(w, np.float32).astype(ml_dtypes.bfloat16)).reshape(k // 32, 32, n)
    amax = np.abs(w).max(1)
    if fmt == "e4m3":
        byte = np.frexp(amax)[1] - 1 + 127 - 7
    else:
        mant, ex = np.frexp(amax / 6.0)
        byte = np.where(mant > 0.5, ex, ex - 1) + 127
    byte = np.clip(np.where(amax > 0, byte, 1), 1, 254)
    scaled = (w * np.exp2(127.0 - byte)[:, None, :]).reshape(k, n).astype(np.float32)
    by_word = np.ascontiguousarray(scaled.reshape(k // 512, 128, 4, n).transpose(0, 1, 3, 2))
    if fmt == "e4m3":
        words = by_word.astype(ml_dtypes.float8_e4m3fn).view(np.uint8)
    else:
        c = by_word.astype(ml_dtypes.float4_e2m1fn).view(np.uint8) & 0xF
        words = (c[..., 0::2] | (c[..., 1::2] << 4)).reshape(k // 512, 128, 2 * n)
    return np.ascontiguousarray(words), np.ascontiguousarray(byte.astype(np.uint8).reshape(k // 512, 16, n))


def unpack_weight(words, scales, fmt):
    g, _, n = scales.shape
    words = np.ascontiguousarray(words).reshape(g, 128, n, -1)
    if fmt == "e4m3":
        vals = words.view(ml_dtypes.float8_e4m3fn).astype(np.float64)
    else:
        nib = np.empty((g, 128, n, 4), np.uint8)
        nib[..., 0::2] = words & 0xF
        nib[..., 1::2] = words >> 4
        vals = E2M1[nib]
    vals = vals * np.repeat(np.exp2(scales.astype(np.float64) - 127.0), 8, axis=1)[..., None]
    return vals.transpose(0, 1, 3, 2).reshape(g * 512, n)


def bf(x):
    return np.asarray(x, np.float32).astype(ml_dtypes.bfloat16)


def planes(Y):
    r, m = Y.shape
    b = f64(bf(Y)).reshape(r // 32, 32, m)
    amax = np.abs(b).max(1)
    byte = np.clip(np.where(amax > 0, np.frexp(amax)[1] - 1 + 127 - 7, 1), 1, 254)
    codes = (b * np.exp2(127.0 - byte)[:, None, :]).reshape(r, m).astype(np.float32).astype(ml_dtypes.float8_e4m3fn).view(np.uint8)
    words = codes.reshape(r // 512, 128, 4, m).transpose(0, 1, 3, 2)
    return np.ascontiguousarray(words), np.ascontiguousarray(byte.astype(np.uint8).reshape(r // 512, 16, m))


D, T, I, Q, E = 512, 2048, 512, 256, 512


def setup_inputs():
    n = np.random.standard_normal
    idx = np.random.permutation(T)[:I]
    fd = mx_kscale(D)
    fi = mx_kscale(I)
    ti = np.ones(T)
    ti[idx] = fi
    ptsp = pack_weight(n((D, T)) / fd[:, None], "e2m1")
    return {
        "query": (n((D, Q)) * 0.25 / np.sqrt(D) * fd[:, None]).astype(np.float32),
        "pts_words": ptsp[0],
        "pts_scales": ptsp[1],
        "kn": np.tile(np.random.uniform(0.5, 1.5, T), (128, 1)).astype(np.float32),
        "qn": (np.random.uniform(0.5, 1.5, (Q, 1))).astype(np.float32),
        "us": (np.random.uniform(0.5, 2.0, (1, I)) * fi).astype(np.float32),
        "coef": (n((E, T)) / ti).astype(np.float32),
        "offs": striped(idx),
    }


def reference(query, pts_words, pts_scales, kn, qn, us, coef, offs):
    idx = unstriped(offs)
    ptsu = unpack_weight(pts_words, pts_scales, "e2m1")
    queryq = mxq(f64(query), 0, "e4m3")
    ptsidxg = ptsu[:, idx]
    a = queryq.T @ ptsidxg
    w = np.exp(a - f64(qn) - f64(kn)[:1][:, idx]) * f64(us)
    wt = w.T
    vt = f64(coef)[:, idx].T
    vtq = mxq(vt, 0, "e4m3")
    wtq = mxq(wt, 0, "e4m3")
    o = vtq.T @ wtq
    words, scales = planes(o)
    return o, words, scales

@@ -1,0 +1,172 @@
+from contextlib import ExitStack
+
+import concourse.mybir as mybir
+from concourse.masks import make_identity
+
+D, T, I, Q, E = 512, 2048, 512, 256, 512
+FLOPS = 2 * D * Q * I + 2 * I * E * Q
+
+F32 = mybir.dt.float32
+BF16 = mybir.dt.bfloat16
+I32 = mybir.dt.int32
+U32 = mybir.dt.uint32
+U16 = mybir.dt.uint16
+U8 = mybir.dt.uint8
+FP8X4 = mybir.dt.float8_e4m3fn_x4
+FP4X4 = mybir.dt.float4_e2m1fn_x4
+ACT = mybir.ActivationFunctionType
+
+P = 128
+PACK = 4
+HALVES = Q // P
+
+
+def tile_attend_kernelridge_pl_kernel(tc, query, pts_words, pts_scales, kn, qn, us, coef, offs, out_0, out_1, out_2):
+    nc = tc.nc
+    with ExitStack() as ctx:
+        sb = ctx.enter_context(tc.tile_pool(name="sb", bufs=1))
+        ps = ctx.enter_context(tc.psum_pool(name="ps", bufs=1))
+
+        offsets = sb.tile([P, I // 16], U16, name="offsets")
+        words_all = sb.tile([P, T], U16, name="words_all", align_bytes=64)
+        scales_all = sb.tile([P, T], U8, name="scales_all", align_bytes=64)
+        kn_all = sb.tile([P, T], F32, name="kn_all", align_bytes=64)
+        query_raw = sb.tile([P, PACK, Q], F32, name="query_raw", align_bytes=64)
+        coef_all = [sb.tile([P, T], F32, name=f"coef_all{t}", align_bytes=64) for t in range(PACK)]
+        qn_col = sb.tile([P, HALVES], F32, name="qn_col")
+        us_col = sb.tile([P, PACK], F32, name="us_col")
+        ident = sb.tile([P, P], F32, name="ident")
+        warm = sb.tile([P, 1], F32, name="warm")
+
+        nc.vector.memset(scales_all[:].bitcast(I32), 0)
+        nc.vector.memset(kn_all[:], 0.0)
+        make_identity(nc, ident[:])
+        nc.scalar.activation(warm[:], ident[:, 0:1], ACT.Exp)
+
+        nc.sync.dma_start(offsets[:], offs)
+        nc.sync.dma_start(words_all[:].bitcast(I32), pts_words[0].bitcast(I32))
+        nc.sync.dma_start(query_raw[:], query.rearrange("(p j) q -> p j q", j=PACK))
+        for quad in range(4):
+            nc.sync.dma_start(
+                scales_all[32 * quad : 32 * quad + 4, :].bitcast(I32),
+                pts_scales[0, 4 * quad : 4 * quad + 4, :].bitcast(I32),
+            )
+        nc.sync.dma_start(kn_all[0:1, :], kn[0:1, :])
+        coef_dealt = coef.rearrange("(p t) n -> p t n", t=PACK)
+        nc.sync.dma_start(coef_all[0][:], coef_dealt[:, 0, :])
+        with nc.allow_non_contiguous_dma(reason="one value of qn a partition for each half of the queries"):
+            nc.sync.dma_start(qn_col[:], qn.rearrange("(h p) o -> p (h o)", p=P))
+        nc.sync.dma_start(us_col[:], us.rearrange("o (p t) -> p (o t)", t=PACK))
+        for t in range(1, PACK):
+            nc.sync.dma_start(coef_all[t][:], coef_dealt[:, t, :])
+
+        words = sb.tile([P, I], U16, name="words", align_bytes=64)
+        scales = sb.tile([P, I], U8, name="scales", align_bytes=64)
+        kn_row = sb.tile([P, I], F32, name="kn_row", align_bytes=64)
+        nc.vector.tensor_copy(words[:], words_all[:].indirect(offsets[:]))
+        nc.vector.tensor_copy(scales[:], scales_all[:].indirect(offsets[:]))
+
+        query_bf = sb.tile([P, Q, PACK], BF16, name="query_bf", align_bytes=64)
+        nc.scalar.copy(
+            query_bf[:].rearrange("p (c i) j -> p c j i", i=4),
+            query_raw[:].rearrange("p j (c i) -> p c j i", i=4),
+        )
+        query_codes = sb.tile([P, Q], U32, name="query_codes", align_bytes=64)
+        query_scales = sb.tile([P, Q], U8, name="query_scales", align_bytes=64)
+        nc.vector.quantize_mx(query_codes[:].bitcast(FP8X4), query_scales[:], query_bf[:].rearrange("p q j -> p (q j)"))
+
+        nc.vector.tensor_copy(kn_row[:], kn_all[:].indirect(offsets[:]))
+
+        gap = []
+        for h in range(HALVES):
+            cols = slice(h * P, (h + 1) * P)
+            dots = ps.tile([P, I], F32, name=f"dots{h}", tag=f"wide{h}")
+            nc.tensor.matmul_mx(
+                dots[:], lhsT=query_codes[:, cols].bitcast(FP8X4), lhsT_scale=query_scales[:, cols],
+                rhs=words[:].bitcast(FP4X4), rhs_scale=scales[:], start=True, stop=True,
+            )
+            gap_h = sb.tile([P, PACK, P], F32, name=f"gap{h}")
+            nc.scalar.activation(
+                gap_h[:], dots[:].rearrange("q (p t) -> q t p", t=PACK), ACT.Identity, bias=qn_col[:, h : h + 1], scale=-1.0
+            )
+            gap.append(gap_h)
+
+        kn_turned = ps.tile([P, PACK, P], F32, name="kn_turned")
+        for t in range(PACK):
+            nc.tensor.transpose(kn_turned[:, t, :], kn_row[:, t::PACK], ident[:])
+        neg_kn = sb.tile([P, PACK], F32, name="neg_kn")
+        nc.scalar.activation(neg_kn[:], kn_turned[:, :, 0], ACT.Copy, scale=-1.0)
+
+        gap_turned = [ps.tile([P, 2, Q], F32, name=f"gap_turned{u}") for u in range(2)]
+        for t in range(PACK):
+            for h in range(HALVES):
+                nc.tensor.transpose(gap_turned[t // 2][:, t % 2, h * P : (h + 1) * P], gap[h][:, t, :], ident[:])
+        kern = sb.tile([P, PACK, Q], F32, name="kern")
+        w_planes = sb.tile([P, PACK, Q], BF16, name="w_planes")
+        for t in range(PACK):
+            nc.scalar.activation(kern[:, t, :], gap_turned[t // 2][:, t % 2, :], ACT.Exp, bias=neg_kn[:, t : t + 1], scale=-1.0)
+        for t in range(PACK):
+            nc.scalar.activation(w_planes[:, t, :], kern[:, t, :], ACT.Copy, scale=us_col[:, t : t + 1])
+        w_bf = sb.tile([P, Q, PACK], BF16, name="w_bf", align_bytes=64)
+        w_codes = sb.tile([P, Q], U32, name="w_codes", align_bytes=64)
+        w_scales = sb.tile([P, Q], U8, name="w_scales", align_bytes=64)
+
+        v_codes = sb.tile([P, PACK, P], U32, name="v_codes", align_bytes=64)
+        v_scales = sb.tile([P, PACK, P], U8, name="v_scales", align_bytes=64)
+
+        def values(t):
+            picked = sb.tile([P, I], BF16, name=f"picked{t}", align_bytes=64)
+            nc.vector.tensor_copy(picked[:], coef_all[t][:].indirect(offsets[:]))
+            pairs = picked[:].bitcast(F32)
+            turned = ps.tile([P, 2, P], F32, name="turned", tag="turned", bufs=3)
+            for u in range(2):
+                nc.tensor.transpose(turned[:, u, :], pairs[:, u::2], ident[:])
+            v_bf = sb.tile([P, P * PACK], BF16, name=f"v_bf{t}", align_bytes=64)
+            nc.scalar.copy(v_bf[:].bitcast(F32).rearrange("p (m u) -> p m u", u=2), turned[:].rearrange("p u m -> p m u"))
+            nc.vector.quantize_mx(v_codes[:, t, :].bitcast(FP8X4), v_scales[:, t, :], v_bf[:])
+
+        sums = [ps.tile([P, PACK, P], F32, name=f"sums{h}", tag=f"wide{h}") for h in range(HALVES)]
+
+        def product(t):
+            for h in range(HALVES):
+                cols = slice(h * P, (h + 1) * P)
+                nc.tensor.matmul_mx(
+                    sums[h][:, t, :], lhsT=v_codes[:, t, :].bitcast(FP8X4), lhsT_scale=v_scales[:, t, :],
+                    rhs=w_codes[:, cols].bitcast(FP8X4), rhs_scale=w_scales[:, cols], start=True, stop=True,
+                )
+
+        result = sb.tile([P, PACK, Q], F32, name="result")
+        out_dealt = out_0.rearrange("(p t) q -> p t q", t=PACK)
+        last = PACK - 1
+
+        for t in range(last):
+            values(t)
+        nc.vector.tensor_copy(
+            w_bf[:].rearrange("p (c i) t -> p c t i", i=4),
+            w_planes[:].rearrange("p t (c i) -> p c t i", i=4),
+        )
+        nc.vector.quantize_mx(w_codes[:].bitcast(FP8X4), w_scales[:], w_bf[:].rearrange("p q t -> p (q t)"))
+        for t in range(last):
+            product(t)
+        for h in range(HALVES):
+            nc.scalar.copy(result[:, :last, h * P : (h + 1) * P], sums[h][:, :last, :])
+        nc.sync.dma_start(out_dealt[:, :last, :], result[:, :last, :])
+
+        values(last)
+        product(last)
+        out_bf = sb.tile([P, Q, PACK], BF16, name="out_bf", align_bytes=64)
+        nc.vector.tensor_copy(out_bf[:, :P, :], sums[0][:].rearrange("p t q -> p q t"))
+        nc.scalar.copy(out_bf[:, P:, :], sums[1][:].rearrange("p t q -> p q t"))
+        for h in reversed(range(HALVES)):
+            nc.scalar.copy(result[:, last, h * P : (h + 1) * P], sums[h][:, last, :])
+        nc.scalar.dma_start(out_dealt[:, last, :], result[:, last, :])
+        out_codes = sb.tile([P, Q], U32, name="out_codes", align_bytes=64)
+        out_scales = sb.tile([P, Q], U8, name="out_scales", align_bytes=64)
+        nc.vector.quantize_mx(out_codes[:].bitcast(FP8X4), out_scales[:], out_bf[:].rearrange("p q t -> p (q t)"))
+        nc.sync.dma_start(out_1[0].rearrange("p q r -> p (q r)").bitcast(I32), out_codes[:].bitcast(I32))
+        for quad in range(4):
+            queue = nc.sync if quad % 2 else nc.scalar
+            queue.dma_start(
+                out_2[0, 4 * quad : 4 * quad + 4, :].bitcast(I32),
+                out_scales[32 * quad : 32 * quad + 4, :].bitcast(I32),
+            )

@@ -1,7 +1,6 @@
 from contextlib import ExitStack
 
 import concourse.mybir as mybir
-from concourse.masks import make_identity
 
 D, T, I, Q, E = 512, 2048, 512, 256, 512
 FLOPS = 2 * D * Q * I + 2 * I * E * Q
@@ -25,22 +24,29 @@ def tile_attend_kernelridge_pl_kernel(tc, query, pts_words, pts_scales, kn, qn, 
     nc = tc.nc
     with ExitStack() as ctx:
         sb = ctx.enter_context(tc.tile_pool(name="sb", bufs=1))
+        shared = ctx.enter_context(tc.tile_pool(name="shared", bufs=1))
         ps = ctx.enter_context(tc.psum_pool(name="ps", bufs=1))
 
         offsets = sb.tile([P, I // 16], U16, name="offsets")
+        zeros = sb.tile([P, P], F32, name="zeros", align_bytes=64)
         words_all = sb.tile([P, T], U16, name="words_all", align_bytes=64)
         scales_all = sb.tile([P, T], U8, name="scales_all", align_bytes=64)
-        kn_all = sb.tile([P, T], F32, name="kn_all", align_bytes=64)
+        kn_all = shared.tile([P, T], F32, name="kn_all", align_bytes=64, offset=8192)
         query_raw = sb.tile([P, PACK, Q], F32, name="query_raw", align_bytes=64)
-        coef_all = [sb.tile([P, T], F32, name=f"coef_all{t}", align_bytes=64) for t in range(PACK)]
-        qn_col = sb.tile([P, HALVES], F32, name="qn_col")
+        coef_all = [shared.tile([P, T], F32, name=f"coef_all{t}", align_bytes=64, offset=16384 + 8192 * t) for t in range(PACK)]
+        rows = sb.tile([P, I], F32, name="rows", align_bytes=64)
         us_col = sb.tile([P, PACK], F32, name="us_col")
         ident = sb.tile([P, P], F32, name="ident")
         warm = sb.tile([P, 1], F32, name="warm")
 
         nc.vector.memset(scales_all[:].bitcast(I32), 0)
-        nc.vector.memset(kn_all[:], 0.0)
-        make_identity(nc, ident[:])
+        nc.vector.memset(kn_all[:].bitcast(I32), 0)
+        nc.gpsimd.memset(zeros[:], 0.0)
+        nc.gpsimd.affine_select(
+            out=ident[:], in_=zeros[:], compare_op=mybir.AluOpType.not_equal, fill=1.0,
+            base=0, pattern=[[-1, P]], channel_multiplier=1,
+        )
+        nc.gpsimd.memset(rows[:], 0.0)
         nc.scalar.activation(warm[:], ident[:, 0:1], ACT.Exp)
 
         nc.sync.dma_start(offsets[:], offs)
@@ -52,21 +58,20 @@ def tile_attend_kernelridge_pl_kernel(tc, query, pts_words, pts_scales, kn, qn, 
                 pts_scales[0, 4 * quad : 4 * quad + 4, :].bitcast(I32),
             )
         nc.sync.dma_start(kn_all[0:1, :], kn[0:1, :])
+        nc.sync.dma_start(rows[0:HALVES, :P], qn.rearrange("(h p) o -> h (p o)", p=P))
         coef_dealt = coef.rearrange("(p t) n -> p t n", t=PACK)
         nc.sync.dma_start(coef_all[0][:], coef_dealt[:, 0, :])
-        with nc.allow_non_contiguous_dma(reason="one value of qn a partition for each half of the queries"):
-            nc.sync.dma_start(qn_col[:], qn.rearrange("(h p) o -> p (h o)", p=P))
-        nc.sync.dma_start(us_col[:], us.rearrange("o (p t) -> p (o t)", t=PACK))
+        nc.sync.dma_start(rows[HALVES : HALVES + 1, :], us)
         for t in range(1, PACK):
             nc.sync.dma_start(coef_all[t][:], coef_dealt[:, t, :])
 
         words = sb.tile([P, I], U16, name="words", align_bytes=64)
         scales = sb.tile([P, I], U8, name="scales", align_bytes=64)
-        kn_row = sb.tile([P, I], F32, name="kn_row", align_bytes=64)
+        kn_row = shared.tile([P, I], F32, name="kn_row", align_bytes=64, offset=4096)
         nc.vector.tensor_copy(words[:], words_all[:].indirect(offsets[:]))
         nc.vector.tensor_copy(scales[:], scales_all[:].indirect(offsets[:]))
 
-        query_bf = sb.tile([P, Q, PACK], BF16, name="query_bf", align_bytes=64)
+        query_bf = shared.tile([P, Q, PACK], BF16, name="query_bf", align_bytes=64, offset=4096)
         nc.scalar.copy(
             query_bf[:].rearrange("p (c i) j -> p c j i", i=4),
             query_raw[:].rearrange("p j (c i) -> p c j i", i=4),
@@ -77,37 +82,53 @@ def tile_attend_kernelridge_pl_kernel(tc, query, pts_words, pts_scales, kn, qn, 
 
         nc.vector.tensor_copy(kn_row[:], kn_all[:].indirect(offsets[:]))
 
-        gap = []
+        qn_turned = ps.tile([P, P], F32, name="qn_turned", tag="turned", bufs=3)
+        nc.tensor.transpose(qn_turned[:], rows[:, :P], ident[:])
+        qn_col = sb.tile([P, HALVES], F32, name="qn_col")
+        nc.scalar.copy(qn_col[:], qn_turned[:, :HALVES])
+
+        dots = []
         for h in range(HALVES):
             cols = slice(h * P, (h + 1) * P)
-            dots = ps.tile([P, I], F32, name=f"dots{h}", tag=f"wide{h}")
+            dots.append(ps.tile([P, I], F32, name=f"dots{h}", tag=f"wide{h}"))
             nc.tensor.matmul_mx(
-                dots[:], lhsT=query_codes[:, cols].bitcast(FP8X4), lhsT_scale=query_scales[:, cols],
+                dots[h][:], lhsT=query_codes[:, cols].bitcast(FP8X4), lhsT_scale=query_scales[:, cols],
                 rhs=words[:].bitcast(FP4X4), rhs_scale=scales[:], start=True, stop=True,
             )
+
+        gap = []
+        for h in range(HALVES):
             gap_h = sb.tile([P, PACK, P], F32, name=f"gap{h}")
             nc.scalar.activation(
-                gap_h[:], dots[:].rearrange("q (p t) -> q t p", t=PACK), ACT.Identity, bias=qn_col[:, h : h + 1], scale=-1.0
+                gap_h[:].rearrange("q t (c i) -> q c t i", i=4),
+                dots[h][:].rearrange("q (c i t) -> q c t i", i=4, t=PACK),
+                ACT.Identity,
+                bias=qn_col[:, h : h + 1],
+                scale=-1.0,
             )
             gap.append(gap_h)
 
-        kn_turned = ps.tile([P, PACK, P], F32, name="kn_turned")
+        norms_turned = ps.tile([P, 8 * PACK + P], F32, name="norms_turned")
         for t in range(PACK):
-            nc.tensor.transpose(kn_turned[:, t, :], kn_row[:, t::PACK], ident[:])
+            nc.tensor.transpose(norms_turned[:, 2 * t : 2 * t + P], kn_row[:, t::PACK], ident[:])
         neg_kn = sb.tile([P, PACK], F32, name="neg_kn")
-        nc.scalar.activation(neg_kn[:], kn_turned[:, :, 0], ACT.Copy, scale=-1.0)
+        nc.scalar.activation(neg_kn[:], norms_turned[:, : 2 * PACK : 2], ACT.Copy, scale=-1.0)
+        for t in range(PACK):
+            nc.tensor.transpose(norms_turned[:, 4 * (PACK + t) : 4 * (PACK + t) + P], rows[:, t::PACK], ident[:])
+
 
         gap_turned = [ps.tile([P, 2, Q], F32, name=f"gap_turned{u}") for u in range(2)]
-        for t in range(PACK):
-            for h in range(HALVES):
+        for h in range(HALVES):
+            for t in range(PACK):
                 nc.tensor.transpose(gap_turned[t // 2][:, t % 2, h * P : (h + 1) * P], gap[h][:, t, :], ident[:])
         kern = sb.tile([P, PACK, Q], F32, name="kern")
-        w_planes = sb.tile([P, PACK, Q], BF16, name="w_planes")
+        w_planes = sb.tile([P, PACK, Q], BF16, name="w_planes", align_bytes=64)
         for t in range(PACK):
             nc.scalar.activation(kern[:, t, :], gap_turned[t // 2][:, t % 2, :], ACT.Exp, bias=neg_kn[:, t : t + 1], scale=-1.0)
+        nc.scalar.copy(us_col[:], norms_turned[:, 4 * PACK + HALVES : 8 * PACK : 4])
         for t in range(PACK):
             nc.scalar.activation(w_planes[:, t, :], kern[:, t, :], ACT.Copy, scale=us_col[:, t : t + 1])
-        w_bf = sb.tile([P, Q, PACK], BF16, name="w_bf", align_bytes=64)
+        w_bf = shared.tile([P, Q, PACK], BF16, name="w_bf", align_bytes=64, offset=16384 + 2 * 8192)
         w_codes = sb.tile([P, Q], U32, name="w_codes", align_bytes=64)
         w_scales = sb.tile([P, Q], U8, name="w_scales", align_bytes=64)
 
@@ -115,16 +136,28 @@ def tile_attend_kernelridge_pl_kernel(tc, query, pts_words, pts_scales, kn, qn, 
         v_scales = sb.tile([P, PACK, P], U8, name="v_scales", align_bytes=64)
 
         def values(t):
-            picked = sb.tile([P, I], BF16, name=f"picked{t}", align_bytes=64)
+            if t == PACK - 1:
+                picked = shared.tile([P, I], BF16, name="picked_last", align_bytes=64, offset=16384 + 2 * 8192 - 512)
+            elif t == 0:
+                picked = shared.tile([P, I], BF16, name="picked_first", align_bytes=64, offset=8192)
+            else:
+                picked = sb.tile([P, I], BF16, name=f"picked{t}", align_bytes=64)
             nc.vector.tensor_copy(picked[:], coef_all[t][:].indirect(offsets[:]))
             pairs = picked[:].bitcast(F32)
-            turned = ps.tile([P, 2, P], F32, name="turned", tag="turned", bufs=3)
+            if t == 0:
+                turned = ps.tile([P, 2, P], F32, name="turned_first", tag="wide1")
+            else:
+                turned = ps.tile([P, 2, P], F32, name="turned", tag="turned", bufs=3)
             for u in range(2):
                 nc.tensor.transpose(turned[:, u, :], pairs[:, u::2], ident[:])
-            v_bf = sb.tile([P, P * PACK], BF16, name=f"v_bf{t}", align_bytes=64)
+            if t == PACK - 2:
+                v_bf = shared.tile([P, P * PACK], BF16, name="v_bf_shared", align_bytes=64, offset=16384 + 2 * 8192 - 1024)
+            else:
+                v_bf = sb.tile([P, P * PACK], BF16, name=f"v_bf{t}", align_bytes=64)
             nc.scalar.copy(v_bf[:].bitcast(F32).rearrange("p (m u) -> p m u", u=2), turned[:].rearrange("p u m -> p m u"))
             nc.vector.quantize_mx(v_codes[:, t, :].bitcast(FP8X4), v_scales[:, t, :], v_bf[:])
 
+        values(0)
         sums = [ps.tile([P, PACK, P], F32, name=f"sums{h}", tag=f"wide{h}") for h in range(HALVES)]
 
         def product(t):
@@ -139,8 +172,8 @@ def tile_attend_kernelridge_pl_kernel(tc, query, pts_words, pts_scales, kn, qn, 
         out_dealt = out_0.rearrange("(p t) q -> p t q", t=PACK)
         last = PACK - 1
 
-        for t in range(last):
-            values(t)
+        values(1)
+        values(2)
         nc.vector.tensor_copy(
             w_bf[:].rearrange("p (c i) t -> p c t i", i=4),
             w_planes[:].rearrange("p t (c i) -> p c t i", i=4),

@@ -34,19 +34,19 @@ def tile_attend_kernelridge_pl_kernel(tc, query, pts_words, pts_scales, kn, qn, 
         kn_all = shared.tile([P, T], F32, name="kn_all", align_bytes=64, offset=8192)
         query_raw = sb.tile([P, PACK, Q], F32, name="query_raw", align_bytes=64)
         coef_all = [shared.tile([P, T], F32, name=f"coef_all{t}", align_bytes=64, offset=16384 + 8192 * t) for t in range(PACK)]
-        rows = sb.tile([P, I], F32, name="rows", align_bytes=64)
+        rows = sb.tile([P, P], F32, name="rows", align_bytes=64)
         us_col = sb.tile([P, PACK], F32, name="us_col")
         ident = sb.tile([P, P], F32, name="ident")
         warm = sb.tile([P, 1], F32, name="warm")
 
         nc.vector.memset(scales_all[:].bitcast(I32), 0)
         nc.vector.memset(kn_all[:].bitcast(I32), 0)
+        nc.vector.memset(rows[:], 0.0)
         nc.gpsimd.memset(zeros[:], 0.0)
         nc.gpsimd.affine_select(
             out=ident[:], in_=zeros[:], compare_op=mybir.AluOpType.not_equal, fill=1.0,
             base=0, pattern=[[-1, P]], channel_multiplier=1,
         )
-        nc.gpsimd.memset(rows[:], 0.0)
         nc.scalar.activation(warm[:], ident[:, 0:1], ACT.Exp)
 
         nc.sync.dma_start(offsets[:], offs)
@@ -57,12 +57,13 @@ def tile_attend_kernelridge_pl_kernel(tc, query, pts_words, pts_scales, kn, qn, 
                 scales_all[32 * quad : 32 * quad + 4, :].bitcast(I32),
                 pts_scales[0, 4 * quad : 4 * quad + 4, :].bitcast(I32),
             )
-        nc.sync.dma_start(kn_all[0:1, :], kn[0:1, :])
-        nc.sync.dma_start(rows[0:HALVES, :P], qn.rearrange("(h p) o -> h (p o)", p=P))
         coef_dealt = coef.rearrange("(p t) n -> p t n", t=PACK)
-        nc.sync.dma_start(coef_all[0][:], coef_dealt[:, 0, :])
-        nc.sync.dma_start(rows[HALVES : HALVES + 1, :], us)
-        for t in range(1, PACK):
+        for t in range(2):
+            nc.sync.dma_start(coef_all[t][:], coef_dealt[:, t, :])
+        nc.sync.dma_start(us_col[:], us.rearrange("o (p t) -> p (o t)", t=PACK))
+        nc.scalar.dma_start(kn_all[0:1, :], kn[0:1, :])
+        nc.scalar.dma_start(rows[0:HALVES, :], qn.rearrange("(h p) o -> h (p o)", p=P))
+        for t in range(2, PACK):
             nc.sync.dma_start(coef_all[t][:], coef_dealt[:, t, :])
 
         words = sb.tile([P, I], U16, name="words", align_bytes=64)
@@ -80,10 +81,12 @@ def tile_attend_kernelridge_pl_kernel(tc, query, pts_words, pts_scales, kn, qn, 
         query_scales = sb.tile([P, Q], U8, name="query_scales", align_bytes=64)
         nc.vector.quantize_mx(query_codes[:].bitcast(FP8X4), query_scales[:], query_bf[:].rearrange("p q j -> p (q j)"))
 
-        nc.vector.tensor_copy(kn_row[:], kn_all[:].indirect(offsets[:]))
+        nc.vector.tensor_copy(
+            kn_row[:].bitcast(U32).rearrange("r (t p) -> r p t", t=PACK), kn_all[:].bitcast(U32).indirect(offsets[:])
+        )
 
-        qn_turned = ps.tile([P, P], F32, name="qn_turned", tag="turned", bufs=3)
-        nc.tensor.transpose(qn_turned[:], rows[:, :P], ident[:])
+        qn_turned = ps.tile([P, P], F32, name="qn_turned", tag="qn_turned")
+        nc.tensor.transpose(qn_turned[:], rows[:], ident[:])
         qn_col = sb.tile([P, HALVES], F32, name="qn_col")
         nc.scalar.copy(qn_col[:], qn_turned[:, :HALVES])
 
@@ -108,13 +111,11 @@ def tile_attend_kernelridge_pl_kernel(tc, query, pts_words, pts_scales, kn, qn, 
             )
             gap.append(gap_h)
 
-        norms_turned = ps.tile([P, 8 * PACK + P], F32, name="norms_turned")
+        norms_turned = ps.tile([P, PACK, P], F32, name="norms_turned")
         for t in range(PACK):
-            nc.tensor.transpose(norms_turned[:, 2 * t : 2 * t + P], kn_row[:, t::PACK], ident[:])
+            nc.tensor.transpose(norms_turned[:, t, :], kn_row[:, t * P : (t + 1) * P], ident[:])
         neg_kn = sb.tile([P, PACK], F32, name="neg_kn")
-        nc.scalar.activation(neg_kn[:], norms_turned[:, : 2 * PACK : 2], ACT.Copy, scale=-1.0)
-        for t in range(PACK):
-            nc.tensor.transpose(norms_turned[:, 4 * (PACK + t) : 4 * (PACK + t) + P], rows[:, t::PACK], ident[:])
+        nc.scalar.activation(neg_kn[:], norms_turned[:, :, 0], ACT.Copy, scale=-1.0)
 
 
         gap_turned = [ps.tile([P, 2, Q], F32, name=f"gap_turned{u}") for u in range(2)]
@@ -125,7 +126,6 @@ def tile_attend_kernelridge_pl_kernel(tc, query, pts_words, pts_scales, kn, qn, 
         w_planes = sb.tile([P, PACK, Q], BF16, name="w_planes", align_bytes=64)
         for t in range(PACK):
             nc.scalar.activation(kern[:, t, :], gap_turned[t // 2][:, t % 2, :], ACT.Exp, bias=neg_kn[:, t : t + 1], scale=-1.0)
-        nc.scalar.copy(us_col[:], norms_turned[:, 4 * PACK + HALVES : 8 * PACK : 4])
         for t in range(PACK):
             nc.scalar.activation(w_planes[:, t, :], kern[:, t, :], ACT.Copy, scale=us_col[:, t : t + 1])
         w_bf = shared.tile([P, Q, PACK], BF16, name="w_bf", align_bytes=64, offset=16384 + 2 * 8192)
@@ -141,13 +141,10 @@ def tile_attend_kernelridge_pl_kernel(tc, query, pts_words, pts_scales, kn, qn, 
             elif t == 0:
                 picked = shared.tile([P, I], BF16, name="picked_first", align_bytes=64, offset=8192)
             else:
-                picked = sb.tile([P, I], BF16, name=f"picked{t}", align_bytes=64)
+                picked = shared.tile([P, I], BF16, name=f"picked{t}", align_bytes=64, offset=16384 + 8192 * (t - 1) + 4096)
             nc.vector.tensor_copy(picked[:], coef_all[t][:].indirect(offsets[:]))
             pairs = picked[:].bitcast(F32)
-            if t == 0:
-                turned = ps.tile([P, 2, P], F32, name="turned_first", tag="wide1")
-            else:
-                turned = ps.tile([P, 2, P], F32, name="turned", tag="turned", bufs=3)
+            turned = ps.tile([P, 2, P], F32, name="turned", tag="wide1" if t < PACK - 1 else "turned_last")
             for u in range(2):
                 nc.tensor.transpose(turned[:, u, :], pairs[:, u::2], ident[:])
             if t == PACK - 2:
@@ -157,7 +154,8 @@ def tile_attend_kernelridge_pl_kernel(tc, query, pts_words, pts_scales, kn, qn, 
             nc.scalar.copy(v_bf[:].bitcast(F32).rearrange("p (m u) -> p m u", u=2), turned[:].rearrange("p u m -> p m u"))
             nc.vector.quantize_mx(v_codes[:, t, :].bitcast(FP8X4), v_scales[:, t, :], v_bf[:])
 
-        values(0)
+        for t in range(PACK - 1):
+            values(t)
         sums = [ps.tile([P, PACK, P], F32, name=f"sums{h}", tag=f"wide{h}") for h in range(HALVES)]
 
         def product(t):
@@ -172,8 +170,6 @@ def tile_attend_kernelridge_pl_kernel(tc, query, pts_words, pts_scales, kn, qn, 
         out_dealt = out_0.rearrange("(p t) q -> p t q", t=PACK)
         last = PACK - 1
 
-        values(1)
-        values(2)
         nc.vector.tensor_copy(
             w_bf[:].rearrange("p (c i) t -> p c t i", i=4),
             w_planes[:].rearrange("p t (c i) -> p c t i", i=4),

@@ -18,6 +18,17 @@ ACT = mybir.ActivationFunctionType
 P = 128
 PACK = 4
 HALVES = Q // P
+QUADRANTS = 4
+RUN = 4
+LAST = PACK - 1
+
+ROW_BYTES = 4 * T
+HALF_ROW = ROW_BYTES // 2
+PICKED_BYTES = 2 * I
+SCALES_AT = 0
+QUERY_AT = HALF_ROW
+KN_AT = ROW_BYTES
+COEF_AT = [(2 + t) * ROW_BYTES for t in range(PACK)]
 
 
 def tile_attend_kernelridge_pl_kernel(tc, query, pts_words, pts_scales, kn, qn, us, coef, offs, out_0, out_1, out_2):
@@ -30,54 +41,55 @@ def tile_attend_kernelridge_pl_kernel(tc, query, pts_words, pts_scales, kn, qn, 
         offsets = sb.tile([P, I // 16], U16, name="offsets")
         zeros = sb.tile([P, P], F32, name="zeros", align_bytes=64)
         words_all = sb.tile([P, T], U16, name="words_all", align_bytes=64)
-        scales_all = sb.tile([P, T], U8, name="scales_all", align_bytes=64)
-        kn_all = shared.tile([P, T], F32, name="kn_all", align_bytes=64, offset=8192)
+        scales_all = shared.tile([P, T], U8, name="scales_all", align_bytes=64, offset=SCALES_AT)
+        kn_all = shared.tile([P, T], F32, name="kn_all", align_bytes=64, offset=KN_AT)
         query_raw = sb.tile([P, PACK, Q], F32, name="query_raw", align_bytes=64)
-        coef_all = [shared.tile([P, T], F32, name=f"coef_all{t}", align_bytes=64, offset=16384 + 8192 * t) for t in range(PACK)]
-        rows = sb.tile([P, P], F32, name="rows", align_bytes=64)
+        coef_all = [shared.tile([P, T], F32, name=f"coef_all{t}", align_bytes=64, offset=COEF_AT[t]) for t in range(PACK)]
+        qn_rows = sb.tile([P, P], F32, name="qn_rows", align_bytes=64)
         us_col = sb.tile([P, PACK], F32, name="us_col")
         ident = sb.tile([P, P], F32, name="ident")
         warm = sb.tile([P, 1], F32, name="warm")
 
+        nc.gpsimd.memset(warm[:], 0.0)
         nc.vector.memset(scales_all[:].bitcast(I32), 0)
         nc.vector.memset(kn_all[:].bitcast(I32), 0)
-        nc.vector.memset(rows[:], 0.0)
+        nc.vector.memset(qn_rows[:], 0.0)
         nc.gpsimd.memset(zeros[:], 0.0)
         nc.gpsimd.affine_select(
             out=ident[:], in_=zeros[:], compare_op=mybir.AluOpType.not_equal, fill=1.0,
             base=0, pattern=[[-1, P]], channel_multiplier=1,
         )
-        nc.scalar.activation(warm[:], ident[:, 0:1], ACT.Exp)
+        nc.scalar.activation(warm[:], warm[:], ACT.Exp)
 
         nc.sync.dma_start(offsets[:], offs)
         nc.sync.dma_start(words_all[:].bitcast(I32), pts_words[0].bitcast(I32))
         nc.sync.dma_start(query_raw[:], query.rearrange("(p j) q -> p j q", j=PACK))
-        for quad in range(4):
+        for quad in range(QUADRANTS):
             nc.sync.dma_start(
                 scales_all[32 * quad : 32 * quad + 4, :].bitcast(I32),
                 pts_scales[0, 4 * quad : 4 * quad + 4, :].bitcast(I32),
             )
-        coef_dealt = coef.rearrange("(p t) n -> p t n", t=PACK)
-        for t in range(2):
-            nc.sync.dma_start(coef_all[t][:], coef_dealt[:, t, :])
+        coef_planes = coef.rearrange("(p t) n -> p t n", t=PACK)
+        for t in range(PACK // 2):
+            nc.sync.dma_start(coef_all[t][:], coef_planes[:, t, :])
         nc.sync.dma_start(us_col[:], us.rearrange("o (p t) -> p (o t)", t=PACK))
         nc.scalar.dma_start(kn_all[0:1, :], kn[0:1, :])
-        nc.scalar.dma_start(rows[0:HALVES, :], qn.rearrange("(h p) o -> h (p o)", p=P))
-        for t in range(2, PACK):
-            nc.sync.dma_start(coef_all[t][:], coef_dealt[:, t, :])
+        nc.scalar.dma_start(qn_rows[0:HALVES, :], qn.rearrange("(h p) o -> h (p o)", p=P))
+        for t in range(PACK // 2, PACK):
+            nc.sync.dma_start(coef_all[t][:], coef_planes[:, t, :])
 
         words = sb.tile([P, I], U16, name="words", align_bytes=64)
         scales = sb.tile([P, I], U8, name="scales", align_bytes=64)
-        kn_row = shared.tile([P, I], F32, name="kn_row", align_bytes=64, offset=4096)
+        kn_row = shared.tile([P, I], F32, name="kn_row", align_bytes=64, offset=QUERY_AT)
         nc.vector.tensor_copy(words[:], words_all[:].indirect(offsets[:]))
         nc.vector.tensor_copy(scales[:], scales_all[:].indirect(offsets[:]))
 
-        query_bf = shared.tile([P, Q, PACK], BF16, name="query_bf", align_bytes=64, offset=4096)
+        query_bf = shared.tile([P, Q, PACK], BF16, name="query_bf", align_bytes=64, offset=QUERY_AT)
         nc.scalar.copy(
-            query_bf[:].rearrange("p (c i) j -> p c j i", i=4),
-            query_raw[:].rearrange("p j (c i) -> p c j i", i=4),
+            query_bf[:].rearrange("p (c i) j -> p c j i", i=RUN),
+            query_raw[:].rearrange("p j (c i) -> p c j i", i=RUN),
         )
-        query_codes = sb.tile([P, Q], U32, name="query_codes", align_bytes=64)
+        query_codes = shared.tile([P, Q], U32, name="query_codes", align_bytes=64, offset=SCALES_AT)
         query_scales = sb.tile([P, Q], U8, name="query_scales", align_bytes=64)
         nc.vector.quantize_mx(query_codes[:].bitcast(FP8X4), query_scales[:], query_bf[:].rearrange("p q j -> p (q j)"))
 
@@ -85,8 +97,8 @@ def tile_attend_kernelridge_pl_kernel(tc, query, pts_words, pts_scales, kn, qn, 
             kn_row[:].bitcast(U32).rearrange("r (t p) -> r p t", t=PACK), kn_all[:].bitcast(U32).indirect(offsets[:])
         )
 
-        qn_turned = ps.tile([P, P], F32, name="qn_turned", tag="qn_turned")
-        nc.tensor.transpose(qn_turned[:], rows[:], ident[:])
+        qn_turned = ps.tile([P, P], F32, name="qn_turned")
+        nc.tensor.transpose(qn_turned[:], qn_rows[:], ident[:])
         qn_col = sb.tile([P, HALVES], F32, name="qn_col")
         nc.scalar.copy(qn_col[:], qn_turned[:, :HALVES])
 
@@ -103,22 +115,21 @@ def tile_attend_kernelridge_pl_kernel(tc, query, pts_words, pts_scales, kn, qn, 
         for h in range(HALVES):
             gap_h = sb.tile([P, PACK, P], F32, name=f"gap{h}")
             nc.scalar.activation(
-                gap_h[:].rearrange("q t (c i) -> q c t i", i=4),
-                dots[h][:].rearrange("q (c i t) -> q c t i", i=4, t=PACK),
+                gap_h[:].rearrange("q t (c i) -> q c t i", i=RUN),
+                dots[h][:].rearrange("q (c i t) -> q c t i", i=RUN, t=PACK),
                 ACT.Identity,
                 bias=qn_col[:, h : h + 1],
                 scale=-1.0,
             )
             gap.append(gap_h)
 
-        norms_turned = ps.tile([P, PACK, P], F32, name="norms_turned")
+        kn_turned = ps.tile([P, PACK, P], F32, name="kn_turned")
         for t in range(PACK):
-            nc.tensor.transpose(norms_turned[:, t, :], kn_row[:, t * P : (t + 1) * P], ident[:])
+            nc.tensor.transpose(kn_turned[:, t, :], kn_row[:, t * P : (t + 1) * P], ident[:])
         neg_kn = sb.tile([P, PACK], F32, name="neg_kn")
-        nc.scalar.activation(neg_kn[:], norms_turned[:, :, 0], ACT.Copy, scale=-1.0)
+        nc.scalar.activation(neg_kn[:], kn_turned[:, :, 0], ACT.Copy, scale=-1.0)
 
-
-        gap_turned = [ps.tile([P, 2, Q], F32, name=f"gap_turned{u}") for u in range(2)]
+        gap_turned = [ps.tile([P, 2, Q], F32, name=f"gap_turned{u}") for u in range(PACK // 2)]
         for h in range(HALVES):
             for t in range(PACK):
                 nc.tensor.transpose(gap_turned[t // 2][:, t % 2, h * P : (h + 1) * P], gap[h][:, t, :], ident[:])
@@ -128,33 +139,31 @@ def tile_attend_kernelridge_pl_kernel(tc, query, pts_words, pts_scales, kn, qn, 
             nc.scalar.activation(kern[:, t, :], gap_turned[t // 2][:, t % 2, :], ACT.Exp, bias=neg_kn[:, t : t + 1], scale=-1.0)
         for t in range(PACK):
             nc.scalar.activation(w_planes[:, t, :], kern[:, t, :], ACT.Copy, scale=us_col[:, t : t + 1])
-        w_bf = shared.tile([P, Q, PACK], BF16, name="w_bf", align_bytes=64, offset=16384 + 2 * 8192)
+        w_bf = shared.tile([P, Q, PACK], BF16, name="w_bf", align_bytes=64, offset=COEF_AT[2])
         w_codes = sb.tile([P, Q], U32, name="w_codes", align_bytes=64)
         w_scales = sb.tile([P, Q], U8, name="w_scales", align_bytes=64)
 
-        v_codes = sb.tile([P, PACK, P], U32, name="v_codes", align_bytes=64)
+        v_codes = shared.tile([P, PACK, P], U32, name="v_codes", align_bytes=64, offset=COEF_AT[2] + HALF_ROW)
         v_scales = sb.tile([P, PACK, P], U8, name="v_scales", align_bytes=64)
 
+        picked_at = [KN_AT, COEF_AT[0] + HALF_ROW, COEF_AT[1] + HALF_ROW, COEF_AT[2] - PICKED_BYTES // 2]
+        third_v_bf_at = COEF_AT[2] - PICKED_BYTES
+
         def values(t):
-            if t == PACK - 1:
-                picked = shared.tile([P, I], BF16, name="picked_last", align_bytes=64, offset=16384 + 2 * 8192 - 512)
-            elif t == 0:
-                picked = shared.tile([P, I], BF16, name="picked_first", align_bytes=64, offset=8192)
-            else:
-                picked = shared.tile([P, I], BF16, name=f"picked{t}", align_bytes=64, offset=16384 + 8192 * (t - 1) + 4096)
+            picked = shared.tile([P, I], BF16, name=f"picked{t}", align_bytes=64, offset=picked_at[t])
             nc.vector.tensor_copy(picked[:], coef_all[t][:].indirect(offsets[:]))
             pairs = picked[:].bitcast(F32)
-            turned = ps.tile([P, 2, P], F32, name="turned", tag="wide1" if t < PACK - 1 else "turned_last")
+            turned = ps.tile([P, 2, P], F32, name="turned", tag="wide1" if t < LAST else "turned_last")
             for u in range(2):
                 nc.tensor.transpose(turned[:, u, :], pairs[:, u::2], ident[:])
-            if t == PACK - 2:
-                v_bf = shared.tile([P, P * PACK], BF16, name="v_bf_shared", align_bytes=64, offset=16384 + 2 * 8192 - 1024)
+            if t == LAST - 1:
+                v_bf = shared.tile([P, P * PACK], BF16, name=f"v_bf{t}", align_bytes=64, offset=third_v_bf_at)
             else:
                 v_bf = sb.tile([P, P * PACK], BF16, name=f"v_bf{t}", align_bytes=64)
             nc.scalar.copy(v_bf[:].bitcast(F32).rearrange("p (m u) -> p m u", u=2), turned[:].rearrange("p u m -> p m u"))
             nc.vector.quantize_mx(v_codes[:, t, :].bitcast(FP8X4), v_scales[:, t, :], v_bf[:])
 
-        for t in range(PACK - 1):
+        for t in range(LAST):
             values(t)
         sums = [ps.tile([P, PACK, P], F32, name=f"sums{h}", tag=f"wide{h}") for h in range(HALVES)]
 
@@ -167,33 +176,33 @@ def tile_attend_kernelridge_pl_kernel(tc, query, pts_words, pts_scales, kn, qn, 
                 )
 
         result = sb.tile([P, PACK, Q], F32, name="result")
-        out_dealt = out_0.rearrange("(p t) q -> p t q", t=PACK)
-        last = PACK - 1
+        out_planes = out_0.rearrange("(p t) q -> p t q", t=PACK)
 
         nc.vector.tensor_copy(
-            w_bf[:].rearrange("p (c i) t -> p c t i", i=4),
-            w_planes[:].rearrange("p t (c i) -> p c t i", i=4),
+            w_bf[:].rearrange("p (c i) t -> p c t i", i=RUN),
+            w_planes[:].rearrange("p t (c i) -> p c t i", i=RUN),
         )
         nc.vector.quantize_mx(w_codes[:].bitcast(FP8X4), w_scales[:], w_bf[:].rearrange("p q t -> p (q t)"))
-        for t in range(last):
+
+        for t in range(LAST):
             product(t)
         for h in range(HALVES):
-            nc.scalar.copy(result[:, :last, h * P : (h + 1) * P], sums[h][:, :last, :])
-        nc.sync.dma_start(out_dealt[:, :last, :], result[:, :last, :])
+            nc.scalar.copy(result[:, :LAST, h * P : (h + 1) * P], sums[h][:, :LAST, :])
+        nc.sync.dma_start(out_planes[:, :LAST, :], result[:, :LAST, :])
 
-        values(last)
-        product(last)
+        values(LAST)
+        product(LAST)
         out_bf = sb.tile([P, Q, PACK], BF16, name="out_bf", align_bytes=64)
         nc.vector.tensor_copy(out_bf[:, :P, :], sums[0][:].rearrange("p t q -> p q t"))
         nc.scalar.copy(out_bf[:, P:, :], sums[1][:].rearrange("p t q -> p q t"))
         for h in reversed(range(HALVES)):
-            nc.scalar.copy(result[:, last, h * P : (h + 1) * P], sums[h][:, last, :])
-        nc.scalar.dma_start(out_dealt[:, last, :], result[:, last, :])
+            nc.scalar.copy(result[:, LAST, h * P : (h + 1) * P], sums[h][:, LAST, :])
+        nc.scalar.dma_start(out_planes[:, LAST, :], result[:, LAST, :])
         out_codes = sb.tile([P, Q], U32, name="out_codes", align_bytes=64)
         out_scales = sb.tile([P, Q], U8, name="out_scales", align_bytes=64)
         nc.vector.quantize_mx(out_codes[:].bitcast(FP8X4), out_scales[:], out_bf[:].rearrange("p q t -> p (q t)"))
         nc.sync.dma_start(out_1[0].rearrange("p q r -> p (q r)").bitcast(I32), out_codes[:].bitcast(I32))
-        for quad in range(4):
+        for quad in range(QUADRANTS):
             queue = nc.sync if quad % 2 else nc.scalar
             queue.dma_start(
                 out_2[0, 4 * quad : 4 * quad + 4, :].bitcast(I32),

@@ -23,12 +23,16 @@ RUN = 4
 LAST = PACK - 1
 
 ROW_BYTES = 4 * T
-HALF_ROW = ROW_BYTES // 2
-PICKED_BYTES = 2 * I
-SCALES_AT = 0
-QUERY_AT = HALF_ROW
-KN_AT = ROW_BYTES
-COEF_AT = [(2 + t) * ROW_BYTES for t in range(PACK)]
+KN_AT = 0
+COEF_AT = [8 * ROW_BYTES, ROW_BYTES // 2, 2 * ROW_BYTES, 4 * ROW_BYTES]
+WORDS_AT = COEF_AT[2] - T
+SCALES_AT = COEF_AT[3] - T // 2
+RAW_AT = 6 * ROW_BYTES
+QUERY_AT = RAW_AT + 4 * PACK * Q
+QN_AT = QUERY_AT + 2 * PACK * Q
+US_AT = QN_AT + 128
+KERN_AT = US_AT + 128
+VBF_AT = 9 * ROW_BYTES
 
 
 def tile_attend_kernelridge_pl_kernel(tc, query, pts_words, pts_scales, kn, qn, us, coef, offs, out_0, out_1, out_2):
@@ -39,29 +43,30 @@ def tile_attend_kernelridge_pl_kernel(tc, query, pts_words, pts_scales, kn, qn, 
         ps = ctx.enter_context(tc.psum_pool(name="ps", bufs=1))
 
         offsets = sb.tile([P, I // 16], U16, name="offsets")
-        zeros = sb.tile([P, P], F32, name="zeros", align_bytes=64)
-        words_all = sb.tile([P, T], U16, name="words_all", align_bytes=64)
+        steps = [shared.tile([P, P // PACK], I32, name=f"steps{t}", align_bytes=64, offset=at) for t, at in enumerate([VBF_AT, QN_AT, COEF_AT[0], US_AT])]
+        words_all = shared.tile([P, T], U16, name="words_all", align_bytes=64, offset=WORDS_AT)
         scales_all = shared.tile([P, T], U8, name="scales_all", align_bytes=64, offset=SCALES_AT)
         kn_all = shared.tile([P, T], F32, name="kn_all", align_bytes=64, offset=KN_AT)
-        query_raw = sb.tile([P, PACK, Q], F32, name="query_raw", align_bytes=64)
-        coef_all = [shared.tile([P, T], F32, name=f"coef_all{t}", align_bytes=64, offset=COEF_AT[t]) for t in range(PACK)]
-        qn_rows = sb.tile([P, P], F32, name="qn_rows", align_bytes=64)
-        us_col = sb.tile([P, PACK], F32, name="us_col")
         ident = sb.tile([P, P], F32, name="ident")
         warm = sb.tile([P, 1], F32, name="warm")
 
         nc.gpsimd.memset(warm[:], 0.0)
+        for t in range(PACK):
+            nc.gpsimd.iota(steps[t][:], pattern=[[1, P // PACK]], base=t * (P // PACK), channel_multiplier=-1)
+        nc.gpsimd.memset(kn_all[: P - 1, : T // 2].bitcast(I32), 0)
         nc.vector.memset(scales_all[:].bitcast(I32), 0)
-        nc.vector.memset(kn_all[:].bitcast(I32), 0)
-        nc.vector.memset(qn_rows[:], 0.0)
-        nc.gpsimd.memset(zeros[:], 0.0)
-        nc.gpsimd.affine_select(
-            out=ident[:], in_=zeros[:], compare_op=mybir.AluOpType.not_equal, fill=1.0,
-            base=0, pattern=[[-1, P]], channel_multiplier=1,
-        )
+        for t in range(PACK):
+            nc.vector.tensor_single_scalar(ident[:, t * (P // PACK) : (t + 1) * (P // PACK)], steps[t][:], 0.0, mybir.AluOpType.is_equal)
+        nc.vector.memset(kn_all[: P - 1, T // 2 :].bitcast(I32), 0)
         nc.scalar.activation(warm[:], warm[:], ACT.Exp)
 
+        query_raw = shared.tile([P, PACK, Q], F32, name="query_raw", align_bytes=64, offset=RAW_AT)
+        coef_all = [shared.tile([P, T], F32, name=f"coef_all{t}", align_bytes=64, offset=COEF_AT[t]) for t in range(PACK)]
+        qn_col = shared.tile([P, HALVES], F32, name="qn_col", align_bytes=64, offset=QN_AT)
+        us_col = shared.tile([P, PACK], F32, name="us_col", align_bytes=64, offset=US_AT)
+        coef_planes = coef.rearrange("(p t) n -> p t n", t=PACK)
         nc.sync.dma_start(offsets[:], offs)
+        nc.sync.dma_start(kn_all[P - 1 :, :], kn[0:1, :])
         nc.sync.dma_start(words_all[:].bitcast(I32), pts_words[0].bitcast(I32))
         nc.sync.dma_start(query_raw[:], query.rearrange("(p j) q -> p j q", j=PACK))
         for quad in range(QUADRANTS):
@@ -69,38 +74,37 @@ def tile_attend_kernelridge_pl_kernel(tc, query, pts_words, pts_scales, kn, qn, 
                 scales_all[32 * quad : 32 * quad + 4, :].bitcast(I32),
                 pts_scales[0, 4 * quad : 4 * quad + 4, :].bitcast(I32),
             )
-        coef_planes = coef.rearrange("(p t) n -> p t n", t=PACK)
-        for t in range(PACK // 2):
-            nc.sync.dma_start(coef_all[t][:], coef_planes[:, t, :])
+        with nc.allow_non_contiguous_dma(reason="one number a partition for each block of queries"):
+            nc.sync.dma_start(qn_col[:], qn.rearrange("(h p) o -> p (h o)", p=P))
+        nc.sync.dma_start(coef_all[0][:], coef_planes[:, 0, :])
         nc.sync.dma_start(us_col[:], us.rearrange("o (p t) -> p (o t)", t=PACK))
-        nc.scalar.dma_start(kn_all[0:1, :], kn[0:1, :])
-        nc.scalar.dma_start(qn_rows[0:HALVES, :], qn.rearrange("(h p) o -> h (p o)", p=P))
-        for t in range(PACK // 2, PACK):
-            nc.sync.dma_start(coef_all[t][:], coef_planes[:, t, :])
 
-        words = sb.tile([P, I], U16, name="words", align_bytes=64)
-        scales = sb.tile([P, I], U8, name="scales", align_bytes=64)
-        kn_row = shared.tile([P, I], F32, name="kn_row", align_bytes=64, offset=QUERY_AT)
+        kn_row = sb.tile([P, I], F32, name="kn_row", align_bytes=64)
+        nc.vector.tensor_copy(
+            kn_row[:].bitcast(U32).rearrange("r (t p) -> r p t", t=PACK), kn_all[:].bitcast(U32).indirect(offsets[:])
+        )
+        nc.sync.dma_start(coef_all[1][:], coef_planes[:, 1, :])
+        kn_turned = ps.tile([P, PACK, P], F32, name="kn_turned")
+        neg_kn = shared.tile([P, PACK], F32, name="neg_kn", align_bytes=64, offset=COEF_AT[1] + ROW_BYTES)
+        for t in range(PACK):
+            nc.tensor.transpose(kn_turned[:, t, :], kn_row[:, t * P : (t + 1) * P], ident[:])
+        nc.scalar.activation(neg_kn[:], kn_turned[:, :, P - 1], ACT.Copy, scale=-1.0)
+
+        words = shared.tile([P, I], U16, name="words", align_bytes=64, offset=KN_AT)
+        scales = shared.tile([P, I], U8, name="scales", align_bytes=64, offset=KN_AT + 2 * I)
         nc.vector.tensor_copy(words[:], words_all[:].indirect(offsets[:]))
+        nc.sync.dma_start(coef_all[2][:], coef_planes[:, 2, :])
         nc.vector.tensor_copy(scales[:], scales_all[:].indirect(offsets[:]))
+        nc.sync.dma_start(coef_all[3][:], coef_planes[:, 3, :])
 
         query_bf = shared.tile([P, Q, PACK], BF16, name="query_bf", align_bytes=64, offset=QUERY_AT)
         nc.scalar.copy(
             query_bf[:].rearrange("p (c i) j -> p c j i", i=RUN),
             query_raw[:].rearrange("p j (c i) -> p c j i", i=RUN),
         )
-        query_codes = shared.tile([P, Q], U32, name="query_codes", align_bytes=64, offset=SCALES_AT)
+        query_codes = shared.tile([P, Q], U32, name="query_codes", align_bytes=64, offset=KN_AT + 4 * I)
         query_scales = sb.tile([P, Q], U8, name="query_scales", align_bytes=64)
         nc.vector.quantize_mx(query_codes[:].bitcast(FP8X4), query_scales[:], query_bf[:].rearrange("p q j -> p (q j)"))
-
-        nc.vector.tensor_copy(
-            kn_row[:].bitcast(U32).rearrange("r (t p) -> r p t", t=PACK), kn_all[:].bitcast(U32).indirect(offsets[:])
-        )
-
-        qn_turned = ps.tile([P, P], F32, name="qn_turned")
-        nc.tensor.transpose(qn_turned[:], qn_rows[:], ident[:])
-        qn_col = sb.tile([P, HALVES], F32, name="qn_col")
-        nc.scalar.copy(qn_col[:], qn_turned[:, :HALVES])
 
         dots = []
         for h in range(HALVES):
@@ -111,6 +115,32 @@ def tile_attend_kernelridge_pl_kernel(tc, query, pts_words, pts_scales, kn, qn, 
                 rhs=words[:].bitcast(FP4X4), rhs_scale=scales[:], start=True, stop=True,
             )
 
+        picked_at = [RAW_AT, COEF_AT[0], COEF_AT[1] + ROW_BYTES - I, COEF_AT[1] + 2 * I]
+        v_bf_at = [VBF_AT + (8 + 2 * t) * I for t in range(PACK)]
+        v_codes_at = [COEF_AT[1], VBF_AT + 2 * I, COEF_AT[3], VBF_AT + 4 * I]
+        banks = ["wide0", "turn1", "turn0", "turn3"]
+        picked, turned, v_bf, v_codes, v_scales = {}, {}, {}, {}, {}
+
+        def gather(t):
+            picked[t] = shared.tile([P, I], BF16, name=f"picked{t}", align_bytes=64, offset=picked_at[t])
+            nc.vector.tensor_copy(picked[t][:], coef_all[t][:].indirect(offsets[:]))
+
+        def turn(t):
+            pairs = picked[t][:].bitcast(F32)
+            turned[t] = ps.tile([P, 2, P], F32, name=f"turned{t}", tag=banks[t])
+            for u in range(2):
+                nc.tensor.transpose(turned[t][:, u, :], pairs[:, u::2], ident[:])
+
+        def empty(t):
+            v_bf[t] = shared.tile([P, P * PACK], BF16, name=f"v_bf{t}", align_bytes=64, offset=v_bf_at[t])
+            nc.scalar.copy(v_bf[t][:].bitcast(F32).rearrange("p (m u) -> p m u", u=2), turned[t][:].rearrange("p u m -> p m u"))
+
+        def quantise(t):
+            v_codes[t] = shared.tile([P, P], U32, name=f"v_codes{t}", align_bytes=64, offset=v_codes_at[t])
+            v_scales[t] = sb.tile([P, P], U8, name=f"v_scales{t}", align_bytes=64)
+            nc.vector.quantize_mx(v_codes[t][:].bitcast(FP8X4), v_scales[t][:], v_bf[t][:])
+
+        gather(0)
         gap = []
         for h in range(HALVES):
             gap_h = sb.tile([P, PACK, P], F32, name=f"gap{h}")
@@ -123,81 +153,68 @@ def tile_attend_kernelridge_pl_kernel(tc, query, pts_words, pts_scales, kn, qn, 
             )
             gap.append(gap_h)
 
-        kn_turned = ps.tile([P, PACK, P], F32, name="kn_turned")
-        for t in range(PACK):
-            nc.tensor.transpose(kn_turned[:, t, :], kn_row[:, t * P : (t + 1) * P], ident[:])
-        neg_kn = sb.tile([P, PACK], F32, name="neg_kn")
-        nc.scalar.activation(neg_kn[:], kn_turned[:, :, 0], ACT.Copy, scale=-1.0)
-
-        gap_turned = [ps.tile([P, 2, Q], F32, name=f"gap_turned{u}") for u in range(PACK // 2)]
+        gap_turned = [ps.tile([P, 2, Q], F32, name=f"gap_turned{u}", tag=f"turn{u}") for u in range(PACK // 2)]
         for h in range(HALVES):
             for t in range(PACK):
                 nc.tensor.transpose(gap_turned[t // 2][:, t % 2, h * P : (h + 1) * P], gap[h][:, t, :], ident[:])
-        kern = sb.tile([P, PACK, Q], F32, name="kern")
-        w_planes = sb.tile([P, PACK, Q], BF16, name="w_planes", align_bytes=64)
+            if h == 0:
+                turn(0)
+        empty(0)
+        kern = shared.tile([P, PACK, Q], F32, name="kern", align_bytes=64, offset=KERN_AT)
         for t in range(PACK):
             nc.scalar.activation(kern[:, t, :], gap_turned[t // 2][:, t % 2, :], ACT.Exp, bias=neg_kn[:, t : t + 1], scale=-1.0)
-        for t in range(PACK):
-            nc.scalar.activation(w_planes[:, t, :], kern[:, t, :], ACT.Copy, scale=us_col[:, t : t + 1])
-        w_bf = shared.tile([P, Q, PACK], BF16, name="w_bf", align_bytes=64, offset=COEF_AT[2])
+
+        gather(1)
+        turn(1)
+        empty(1)
+        quantise(0)
+        w_bf = shared.tile([P, Q, PACK], BF16, name="w_bf", align_bytes=64, offset=COEF_AT[1] + 2 * I)
+        nc.vector.tensor_tensor(
+            w_bf[:].rearrange("p (c i) t -> p c t i", i=RUN),
+            kern[:].rearrange("p t (c i) -> p c t i", i=RUN),
+            us_col[:].unsqueeze(1).unsqueeze(3).to_broadcast([P, Q // RUN, PACK, RUN]),
+            mybir.AluOpType.mult,
+        )
+        gather(2)
         w_codes = sb.tile([P, Q], U32, name="w_codes", align_bytes=64)
         w_scales = sb.tile([P, Q], U8, name="w_scales", align_bytes=64)
+        nc.vector.quantize_mx(w_codes[:].bitcast(FP8X4), w_scales[:], w_bf[:].rearrange("p q t -> p (q t)"))
+        quantise(1)
+        turn(2)
+        empty(2)
+        gather(3)
 
-        v_codes = shared.tile([P, PACK, P], U32, name="v_codes", align_bytes=64, offset=COEF_AT[2] + HALF_ROW)
-        v_scales = sb.tile([P, PACK, P], U8, name="v_scales", align_bytes=64)
-
-        picked_at = [KN_AT, COEF_AT[0] + HALF_ROW, COEF_AT[1] + HALF_ROW, COEF_AT[2] - PICKED_BYTES // 2]
-        third_v_bf_at = COEF_AT[2] - PICKED_BYTES
-
-        def values(t):
-            picked = shared.tile([P, I], BF16, name=f"picked{t}", align_bytes=64, offset=picked_at[t])
-            nc.vector.tensor_copy(picked[:], coef_all[t][:].indirect(offsets[:]))
-            pairs = picked[:].bitcast(F32)
-            turned = ps.tile([P, 2, P], F32, name="turned", tag="wide1" if t < LAST else "turned_last")
-            for u in range(2):
-                nc.tensor.transpose(turned[:, u, :], pairs[:, u::2], ident[:])
-            if t == LAST - 1:
-                v_bf = shared.tile([P, P * PACK], BF16, name=f"v_bf{t}", align_bytes=64, offset=third_v_bf_at)
-            else:
-                v_bf = sb.tile([P, P * PACK], BF16, name=f"v_bf{t}", align_bytes=64)
-            nc.scalar.copy(v_bf[:].bitcast(F32).rearrange("p (m u) -> p m u", u=2), turned[:].rearrange("p u m -> p m u"))
-            nc.vector.quantize_mx(v_codes[:, t, :].bitcast(FP8X4), v_scales[:, t, :], v_bf[:])
-
-        for t in range(LAST):
-            values(t)
         sums = [ps.tile([P, PACK, P], F32, name=f"sums{h}", tag=f"wide{h}") for h in range(HALVES)]
 
         def product(t):
             for h in range(HALVES):
                 cols = slice(h * P, (h + 1) * P)
                 nc.tensor.matmul_mx(
-                    sums[h][:, t, :], lhsT=v_codes[:, t, :].bitcast(FP8X4), lhsT_scale=v_scales[:, t, :],
+                    sums[h][:, t, :], lhsT=v_codes[t][:].bitcast(FP8X4), lhsT_scale=v_scales[t][:],
                     rhs=w_codes[:, cols].bitcast(FP8X4), rhs_scale=w_scales[:, cols], start=True, stop=True,
                 )
 
-        result = sb.tile([P, PACK, Q], F32, name="result")
+        result = [sb.tile([P, 2, Q], F32, name=f"result{u}") for u in range(2)]
         out_planes = out_0.rearrange("(p t) q -> p t q", t=PACK)
 
-        nc.vector.tensor_copy(
-            w_bf[:].rearrange("p (c i) t -> p c t i", i=RUN),
-            w_planes[:].rearrange("p t (c i) -> p c t i", i=RUN),
-        )
-        nc.vector.quantize_mx(w_codes[:].bitcast(FP8X4), w_scales[:], w_bf[:].rearrange("p q t -> p (q t)"))
-
-        for t in range(LAST):
-            product(t)
+        product(0)
+        product(1)
         for h in range(HALVES):
-            nc.scalar.copy(result[:, :LAST, h * P : (h + 1) * P], sums[h][:, :LAST, :])
-        nc.sync.dma_start(out_planes[:, :LAST, :], result[:, :LAST, :])
+            nc.scalar.copy(result[0][:, :, h * P : (h + 1) * P], sums[h][:, :2, :])
+        nc.sync.dma_start(out_planes[:, :2, :], result[0][:])
 
-        values(LAST)
-        product(LAST)
+        turn(3)
+        empty(3)
+        quantise(2)
+        product(2)
+        quantise(3)
+        product(3)
         out_bf = sb.tile([P, Q, PACK], BF16, name="out_bf", align_bytes=64)
         nc.vector.tensor_copy(out_bf[:, :P, :], sums[0][:].rearrange("p t q -> p q t"))
         nc.scalar.copy(out_bf[:, P:, :], sums[1][:].rearrange("p t q -> p q t"))
         for h in reversed(range(HALVES)):
-            nc.scalar.copy(result[:, LAST, h * P : (h + 1) * P], sums[h][:, LAST, :])
-        nc.scalar.dma_start(out_planes[:, LAST, :], result[:, LAST, :])
+            nc.scalar.copy(result[1][:, :, h * P : (h + 1) * P], sums[h][:, 2:, :])
+        nc.scalar.dma_start(out_planes[:, 2:, :], result[1][:])
         out_codes = sb.tile([P, Q], U32, name="out_codes", align_bytes=64)
         out_scales = sb.tile([P, Q], U8, name="out_scales", align_bytes=64)
         nc.vector.quantize_mx(out_codes[:].bitcast(FP8X4), out_scales[:], out_bf[:].rearrange("p q t -> p (q t)"))

@@ -66,7 +66,7 @@ def tile_attend_kernelridge_pl_kernel(tc, query, pts_words, pts_scales, kn, qn, 
         us_col = shared.tile([P, PACK], F32, name="us_col", align_bytes=64, offset=US_AT)
         coef_planes = coef.rearrange("(p t) n -> p t n", t=PACK)
         nc.sync.dma_start(offsets[:], offs)
-        nc.sync.dma_start(kn_all[P - 1 :, :], kn[0:1, :])
+        nc.scalar.dma_start(kn_all[P - 1 :, :], kn[0:1, :])
         nc.sync.dma_start(words_all[:].bitcast(I32), pts_words[0].bitcast(I32))
         nc.sync.dma_start(query_raw[:], query.rearrange("(p j) q -> p j q", j=PACK))
         for quad in range(QUADRANTS):
@@ -115,9 +115,9 @@ def tile_attend_kernelridge_pl_kernel(tc, query, pts_words, pts_scales, kn, qn, 
                 rhs=words[:].bitcast(FP4X4), rhs_scale=scales[:], start=True, stop=True,
             )
 
-        picked_at = [RAW_AT, COEF_AT[0], COEF_AT[1] + ROW_BYTES - I, COEF_AT[1] + 2 * I]
+        picked_at = [RAW_AT, COEF_AT[0], KERN_AT, KERN_AT + 2 * I]
         v_bf_at = [VBF_AT + (8 + 2 * t) * I for t in range(PACK)]
-        v_codes_at = [COEF_AT[1], VBF_AT + 2 * I, COEF_AT[3], VBF_AT + 4 * I]
+        v_codes_at = [COEF_AT[1], COEF_AT[1] + I, COEF_AT[3], VBF_AT + 4 * I]
         banks = ["wide0", "turn1", "turn0", "turn3"]
         picked, turned, v_bf, v_codes, v_scales = {}, {}, {}, {}, {}
 
@@ -167,7 +167,6 @@ def tile_attend_kernelridge_pl_kernel(tc, query, pts_words, pts_scales, kn, qn, 
         gather(1)
         turn(1)
         empty(1)
-        quantise(0)
         w_bf = shared.tile([P, Q, PACK], BF16, name="w_bf", align_bytes=64, offset=COEF_AT[1] + 2 * I)
         nc.vector.tensor_tensor(
             w_bf[:].rearrange("p (c i) t -> p c t i", i=RUN),
@@ -175,11 +174,12 @@ def tile_attend_kernelridge_pl_kernel(tc, query, pts_words, pts_scales, kn, qn, 
             us_col[:].unsqueeze(1).unsqueeze(3).to_broadcast([P, Q // RUN, PACK, RUN]),
             mybir.AluOpType.mult,
         )
-        gather(2)
+        quantise(0)
+        quantise(1)
         w_codes = sb.tile([P, Q], U32, name="w_codes", align_bytes=64)
         w_scales = sb.tile([P, Q], U8, name="w_scales", align_bytes=64)
         nc.vector.quantize_mx(w_codes[:].bitcast(FP8X4), w_scales[:], w_bf[:].rearrange("p q t -> p (q t)"))
-        quantise(1)
+        gather(2)
         turn(2)
         empty(2)
         gather(3)
@@ -194,15 +194,14 @@ def tile_attend_kernelridge_pl_kernel(tc, query, pts_words, pts_scales, kn, qn, 
                     rhs=w_codes[:, cols].bitcast(FP8X4), rhs_scale=w_scales[:, cols], start=True, stop=True,
                 )
 
-        result = [sb.tile([P, 2, Q], F32, name=f"result{u}") for u in range(2)]
         out_planes = out_0.rearrange("(p t) q -> p t q", t=PACK)
 
+        result = [sb.tile([P, 2, Q], F32, name=f"result{u}") for u in range(2)]
         product(0)
         product(1)
         for h in range(HALVES):
             nc.scalar.copy(result[0][:, :, h * P : (h + 1) * P], sums[h][:, :2, :])
         nc.sync.dma_start(out_planes[:, :2, :], result[0][:])
-
         turn(3)
         empty(3)
         quantise(2)
@@ -210,10 +209,10 @@ def tile_attend_kernelridge_pl_kernel(tc, query, pts_words, pts_scales, kn, qn, 
         quantise(3)
         product(3)
         out_bf = sb.tile([P, Q, PACK], BF16, name="out_bf", align_bytes=64)
-        nc.vector.tensor_copy(out_bf[:, :P, :], sums[0][:].rearrange("p t q -> p q t"))
-        nc.scalar.copy(out_bf[:, P:, :], sums[1][:].rearrange("p t q -> p q t"))
-        for h in reversed(range(HALVES)):
-            nc.scalar.copy(result[1][:, :, h * P : (h + 1) * P], sums[h][:, 2:, :])
+        for h, copy in enumerate([nc.vector.tensor_copy, nc.scalar.copy]):
+            cols = slice(h * P, (h + 1) * P)
+            copy(out_bf[:, cols, :], sums[h][:].rearrange("p t q -> p q t"))
+            copy(result[1][:, :, cols], sums[h][:, 2:, :])
         nc.scalar.dma_start(out_planes[:, 2:, :], result[1][:])
         out_codes = sb.tile([P, Q], U32, name="out_codes", align_bytes=64)
         out_scales = sb.tile([P, Q], U8, name="out_scales", align_bytes=64)

@@ -30,7 +30,7 @@ SCALES_AT = COEF_AT[3] - T // 2
 RAW_AT = 6 * ROW_BYTES
 QUERY_AT = RAW_AT + 4 * PACK * Q
 QN_AT = QUERY_AT + 2 * PACK * Q
-US_AT = QN_AT + 128
+US_AT = QN_AT + 4 * P
 KERN_AT = US_AT + 128
 VBF_AT = 9 * ROW_BYTES
 
@@ -48,9 +48,7 @@ def tile_attend_kernelridge_pl_kernel(tc, query, pts_words, pts_scales, kn, qn, 
         scales_all = shared.tile([P, T], U8, name="scales_all", align_bytes=64, offset=SCALES_AT)
         kn_all = shared.tile([P, T], F32, name="kn_all", align_bytes=64, offset=KN_AT)
         ident = sb.tile([P, P], F32, name="ident")
-        warm = sb.tile([P, 1], F32, name="warm")
 
-        nc.gpsimd.memset(warm[:], 0.0)
         for t in range(PACK):
             nc.gpsimd.iota(steps[t][:], pattern=[[1, P // PACK]], base=t * (P // PACK), channel_multiplier=-1)
         nc.gpsimd.memset(kn_all[: P - 1, : T // 2].bitcast(I32), 0)
@@ -58,24 +56,20 @@ def tile_attend_kernelridge_pl_kernel(tc, query, pts_words, pts_scales, kn, qn, 
         for t in range(PACK):
             nc.vector.tensor_single_scalar(ident[:, t * (P // PACK) : (t + 1) * (P // PACK)], steps[t][:], 0.0, mybir.AluOpType.is_equal)
         nc.vector.memset(kn_all[: P - 1, T // 2 :].bitcast(I32), 0)
-        nc.scalar.activation(warm[:], warm[:], ACT.Exp)
 
         query_raw = shared.tile([P, PACK, Q], F32, name="query_raw", align_bytes=64, offset=RAW_AT)
         coef_all = [shared.tile([P, T], F32, name=f"coef_all{t}", align_bytes=64, offset=COEF_AT[t]) for t in range(PACK)]
-        qn_col = shared.tile([P, HALVES], F32, name="qn_col", align_bytes=64, offset=QN_AT)
+        qn_rows = shared.tile([P, P], F32, name="qn_rows", align_bytes=64, offset=QN_AT)
         us_col = shared.tile([P, PACK], F32, name="us_col", align_bytes=64, offset=US_AT)
         coef_planes = coef.rearrange("(p t) n -> p t n", t=PACK)
         nc.sync.dma_start(offsets[:], offs)
         nc.scalar.dma_start(kn_all[P - 1 :, :], kn[0:1, :])
         nc.sync.dma_start(words_all[:].bitcast(I32), pts_words[0].bitcast(I32))
         nc.sync.dma_start(query_raw[:], query.rearrange("(p j) q -> p j q", j=PACK))
-        for quad in range(QUADRANTS):
-            nc.sync.dma_start(
-                scales_all[32 * quad : 32 * quad + 4, :].bitcast(I32),
-                pts_scales[0, 4 * quad : 4 * quad + 4, :].bitcast(I32),
-            )
-        with nc.allow_non_contiguous_dma(reason="one number a partition for each block of queries"):
-            nc.sync.dma_start(qn_col[:], qn.rearrange("(h p) o -> p (h o)", p=P))
+        for row in range(4):
+            nc.sync.dma_start(scales_all[row::32, :].bitcast(I32), pts_scales[0, row::4, :].bitcast(I32))
+        nc.sync.dma_start(qn_rows[P - HALVES :, :], qn.rearrange("(h p) o -> h (p o)", p=P))
+        nc.gpsimd.memset(qn_rows[: P - HALVES, :], 0.0)
         nc.sync.dma_start(coef_all[0][:], coef_planes[:, 0, :])
         nc.sync.dma_start(us_col[:], us.rearrange("o (p t) -> p (o t)", t=PACK))
 
@@ -90,6 +84,11 @@ def tile_attend_kernelridge_pl_kernel(tc, query, pts_words, pts_scales, kn, qn, 
             nc.tensor.transpose(kn_turned[:, t, :], kn_row[:, t * P : (t + 1) * P], ident[:])
         nc.scalar.activation(neg_kn[:], kn_turned[:, :, P - 1], ACT.Copy, scale=-1.0)
 
+        qn_turned = ps.tile([P, P], F32, name="qn_turned")
+        nc.tensor.transpose(qn_turned[:], qn_rows[:], ident[:])
+        qn_col = sb.tile([P, HALVES], F32, name="qn_col")
+        nc.scalar.copy(qn_col[:], qn_turned[:, P - HALVES :])
+
         words = shared.tile([P, I], U16, name="words", align_bytes=64, offset=KN_AT)
         scales = shared.tile([P, I], U8, name="scales", align_bytes=64, offset=KN_AT + 2 * I)
         nc.vector.tensor_copy(words[:], words_all[:].indirect(offsets[:]))
@@ -103,7 +102,7 @@ def tile_attend_kernelridge_pl_kernel(tc, query, pts_words, pts_scales, kn, qn, 
             query_raw[:].rearrange("p j (c i) -> p c j i", i=RUN),
         )
         query_codes = shared.tile([P, Q], U32, name="query_codes", align_bytes=64, offset=KN_AT + 4 * I)
-        query_scales = sb.tile([P, Q], U8, name="query_scales", align_bytes=64)
+        query_scales = shared.tile([P, Q], U8, name="query_scales", align_bytes=64, offset=QN_AT)
         nc.vector.quantize_mx(query_codes[:].bitcast(FP8X4), query_scales[:], query_bf[:].rearrange("p q j -> p (q j)"))
 
         dots = []

@@ -24,12 +24,14 @@ LAST = PACK - 1
 
 ROW_BYTES = 4 * T
 KN_AT = 0
-COEF_AT = [8 * ROW_BYTES, ROW_BYTES // 2, 2 * ROW_BYTES, 4 * ROW_BYTES]
-WORDS_AT = COEF_AT[2] - T
-SCALES_AT = COEF_AT[3] - T // 2
+KN_ROW_AT = 2 * ROW_BYTES
+SCALES_AT = KN_ROW_AT + 2 * I
+COEF_AT = [8 * ROW_BYTES, KN_ROW_AT + 4 * I, ROW_BYTES // 2, 4 * ROW_BYTES]
+WORDS_AT = COEF_AT[3] - T
+ROWS = D // 32
 RAW_AT = 6 * ROW_BYTES
-QUERY_AT = RAW_AT + 4 * PACK * Q
-QN_AT = QUERY_AT + 2 * PACK * Q
+QUERY_AT = 11 * ROW_BYTES
+QN_AT = RAW_AT + 4 * PACK * Q
 US_AT = QN_AT + 4 * P
 KERN_AT = US_AT + 128
 VBF_AT = 9 * ROW_BYTES
@@ -43,66 +45,71 @@ def tile_attend_kernelridge_pl_kernel(tc, query, pts_words, pts_scales, kn, qn, 
         ps = ctx.enter_context(tc.psum_pool(name="ps", bufs=1))
 
         offsets = sb.tile([P, I // 16], U16, name="offsets")
-        steps = [shared.tile([P, P // PACK], I32, name=f"steps{t}", align_bytes=64, offset=at) for t, at in enumerate([VBF_AT, QN_AT, COEF_AT[0], US_AT])]
         words_all = shared.tile([P, T], U16, name="words_all", align_bytes=64, offset=WORDS_AT)
         scales_all = shared.tile([P, T], U8, name="scales_all", align_bytes=64, offset=SCALES_AT)
         kn_all = shared.tile([P, T], F32, name="kn_all", align_bytes=64, offset=KN_AT)
-        ident = sb.tile([P, P], F32, name="ident")
-
-        for t in range(PACK):
-            nc.gpsimd.iota(steps[t][:], pattern=[[1, P // PACK]], base=t * (P // PACK), channel_multiplier=-1)
-        nc.gpsimd.memset(kn_all[: P - 1, : T // 2].bitcast(I32), 0)
-        nc.vector.memset(scales_all[:].bitcast(I32), 0)
-        for t in range(PACK):
-            nc.vector.tensor_single_scalar(ident[:, t * (P // PACK) : (t + 1) * (P // PACK)], steps[t][:], 0.0, mybir.AluOpType.is_equal)
-        nc.vector.memset(kn_all[: P - 1, T // 2 :].bitcast(I32), 0)
-
         query_raw = shared.tile([P, PACK, Q], F32, name="query_raw", align_bytes=64, offset=RAW_AT)
         coef_all = [shared.tile([P, T], F32, name=f"coef_all{t}", align_bytes=64, offset=COEF_AT[t]) for t in range(PACK)]
         qn_rows = shared.tile([P, P], F32, name="qn_rows", align_bytes=64, offset=QN_AT)
-        us_col = shared.tile([P, PACK], F32, name="us_col", align_bytes=64, offset=US_AT)
+        zeros = sb.tile([P, P], F32, name="zeros")
+        ident = sb.tile([P, P], F32, name="ident")
+        scales = sb.tile([P, I], U8, name="scales", align_bytes=64)
+
         coef_planes = coef.rearrange("(p t) n -> p t n", t=PACK)
         nc.sync.dma_start(offsets[:], offs)
+        nc.sync.dma_start(scales_all[P - ROWS :, :].bitcast(I32), pts_scales[0].bitcast(I32))
         nc.scalar.dma_start(kn_all[P - 1 :, :], kn[0:1, :])
         nc.sync.dma_start(words_all[:].bitcast(I32), pts_words[0].bitcast(I32))
         nc.sync.dma_start(query_raw[:], query.rearrange("(p j) q -> p j q", j=PACK))
-        for row in range(4):
-            nc.sync.dma_start(scales_all[row::32, :].bitcast(I32), pts_scales[0, row::4, :].bitcast(I32))
         nc.sync.dma_start(qn_rows[P - HALVES :, :], qn.rearrange("(h p) o -> h (p o)", p=P))
-        nc.gpsimd.memset(qn_rows[: P - HALVES, :], 0.0)
         nc.sync.dma_start(coef_all[0][:], coef_planes[:, 0, :])
-        nc.sync.dma_start(us_col[:], us.rearrange("o (p t) -> p (o t)", t=PACK))
 
-        kn_row = sb.tile([P, I], F32, name="kn_row", align_bytes=64)
+        nc.gpsimd.memset(kn_all[: P - 1, : T // 2].bitcast(I32), 0)
+        nc.gpsimd.memset(zeros[:], 0.0)
+        nc.gpsimd.affine_select(
+            out=ident[:], in_=zeros[:], compare_op=mybir.AluOpType.not_equal, fill=1.0,
+            base=0, pattern=[[-1, P]], channel_multiplier=1,
+        )
+        nc.gpsimd.memset(qn_rows[: P - HALVES, :], 0.0)
+        nc.vector.memset(scales_all[: P - ROWS, :].bitcast(I32), 0)
+        nc.vector.memset(kn_all[: P - 1, T // 2 :].bitcast(I32), 0)
+        nc.vector.memset(scales[:].bitcast(I32), 0)
+
+        scale_rows = sb.tile([P, I], U8, name="scale_rows", align_bytes=64)
+        nc.vector.tensor_copy(scale_rows[:], scales_all[:].indirect(offsets[:]))
+        for row in range(4):
+            nc.sync.dma_start(scales[row::32, :].bitcast(I32), scale_rows[P - ROWS + row :: 4, :].bitcast(I32))
+        nc.sync.dma_start(coef_all[1][:], coef_planes[:, 1, :])
+
+        kn_row = shared.tile([P, I], F32, name="kn_row", align_bytes=64, offset=KN_ROW_AT)
         nc.vector.tensor_copy(
             kn_row[:].bitcast(U32).rearrange("r (t p) -> r p t", t=PACK), kn_all[:].bitcast(U32).indirect(offsets[:])
         )
-        nc.sync.dma_start(coef_all[1][:], coef_planes[:, 1, :])
+        us_col = shared.tile([P, PACK], F32, name="us_col", align_bytes=64, offset=KN_AT + 6 * I)
+        nc.sync.dma_start(us_col[:], us.rearrange("o (p t) -> p (o t)", t=PACK))
+        nc.sync.dma_start(coef_all[2][:], coef_planes[:, 2, :])
+        query_bf = shared.tile([P, Q, PACK], BF16, name="query_bf", align_bytes=64, offset=QUERY_AT)
+        nc.scalar.copy(
+            query_bf[:].rearrange("p (c i) j -> p c j i", i=RUN),
+            query_raw[:].rearrange("p j (c i) -> p c j i", i=RUN),
+        )
         kn_turned = ps.tile([P, PACK, P], F32, name="kn_turned")
-        neg_kn = shared.tile([P, PACK], F32, name="neg_kn", align_bytes=64, offset=COEF_AT[1] + ROW_BYTES)
+        neg_kn = shared.tile([P, PACK], F32, name="neg_kn", align_bytes=64, offset=RAW_AT + 4 * I)
         for t in range(PACK):
             nc.tensor.transpose(kn_turned[:, t, :], kn_row[:, t * P : (t + 1) * P], ident[:])
         nc.scalar.activation(neg_kn[:], kn_turned[:, :, P - 1], ACT.Copy, scale=-1.0)
 
         qn_turned = ps.tile([P, P], F32, name="qn_turned")
         nc.tensor.transpose(qn_turned[:], qn_rows[:], ident[:])
-        qn_col = sb.tile([P, HALVES], F32, name="qn_col")
+        qn_col = shared.tile([P, HALVES], F32, name="qn_col", align_bytes=64, offset=RAW_AT + 5 * I)
         nc.scalar.copy(qn_col[:], qn_turned[:, P - HALVES :])
 
         words = shared.tile([P, I], U16, name="words", align_bytes=64, offset=KN_AT)
-        scales = shared.tile([P, I], U8, name="scales", align_bytes=64, offset=KN_AT + 2 * I)
         nc.vector.tensor_copy(words[:], words_all[:].indirect(offsets[:]))
-        nc.sync.dma_start(coef_all[2][:], coef_planes[:, 2, :])
-        nc.vector.tensor_copy(scales[:], scales_all[:].indirect(offsets[:]))
         nc.sync.dma_start(coef_all[3][:], coef_planes[:, 3, :])
 
-        query_bf = shared.tile([P, Q, PACK], BF16, name="query_bf", align_bytes=64, offset=QUERY_AT)
-        nc.scalar.copy(
-            query_bf[:].rearrange("p (c i) j -> p c j i", i=RUN),
-            query_raw[:].rearrange("p j (c i) -> p c j i", i=RUN),
-        )
         query_codes = shared.tile([P, Q], U32, name="query_codes", align_bytes=64, offset=KN_AT + 4 * I)
-        query_scales = shared.tile([P, Q], U8, name="query_scales", align_bytes=64, offset=QN_AT)
+        query_scales = shared.tile([P, Q], U8, name="query_scales", align_bytes=64, offset=QN_AT + Q)
         nc.vector.quantize_mx(query_codes[:].bitcast(FP8X4), query_scales[:], query_bf[:].rearrange("p q j -> p (q j)"))
 
         dots = []
@@ -114,7 +121,7 @@ def tile_attend_kernelridge_pl_kernel(tc, query, pts_words, pts_scales, kn, qn, 
                 rhs=words[:].bitcast(FP4X4), rhs_scale=scales[:], start=True, stop=True,
             )
 
-        picked_at = [RAW_AT, COEF_AT[0], KERN_AT, KERN_AT + 2 * I]
+        picked_at = [QN_AT + Q - 2 * I, COEF_AT[0], KERN_AT, KERN_AT + 2 * I]
         v_bf_at = [VBF_AT + (8 + 2 * t) * I for t in range(PACK)]
         v_codes_at = [COEF_AT[1], COEF_AT[1] + I, COEF_AT[3], VBF_AT + 4 * I]
         banks = ["wide0", "turn1", "turn0", "turn3"]

@@ -19,23 +19,31 @@ P = 128
 PACK = 4
 HALVES = Q // P
 QUADRANTS = 4
+LIVE = 4
+ROWS = QUADRANTS * LIVE
 RUN = 4
-LAST = PACK - 1
 
 ROW_BYTES = 4 * T
+PICKED_BYTES = 2 * I
 KN_AT = 0
 KN_ROW_AT = 2 * ROW_BYTES
 SCALES_AT = KN_ROW_AT + 2 * I
-COEF_AT = [8 * ROW_BYTES, KN_ROW_AT + 4 * I, ROW_BYTES // 2, 4 * ROW_BYTES]
-WORDS_AT = COEF_AT[3] - T
-ROWS = D // 32
+COEF_AT = [8 * ROW_BYTES, KN_ROW_AT + 4 * I, 4 * ROW_BYTES, KN_AT + ROW_BYTES // 2]
+WORDS_AT = COEF_AT[2] - T
+QUERY_CODES_AT = KN_AT + 4 * I
+US_AT = WORDS_AT
 RAW_AT = 6 * ROW_BYTES
-QUERY_AT = 11 * ROW_BYTES
+NEG_KN_AT = RAW_AT + 4 * I
+QN_COL_AT = RAW_AT + 5 * I
 QN_AT = RAW_AT + 4 * PACK * Q
-US_AT = QN_AT + 4 * P
-KERN_AT = US_AT + 128
-VBF_AT = 9 * ROW_BYTES
-
+QUERY_SCALES_AT = QN_AT + Q
+KERN_AT = QN_AT + 4 * P + P
+FREE_AT = 9 * ROW_BYTES
+QUERY_AT = 11 * ROW_BYTES
+PICKED_AT = [QUERY_SCALES_AT - PICKED_BYTES, COEF_AT[0], KERN_AT, KERN_AT + PICKED_BYTES]
+V_CODES_AT = [COEF_AT[1], COEF_AT[1] + 4 * P, COEF_AT[3], FREE_AT + 2 * PICKED_BYTES]
+W_AT = COEF_AT[1] + PICKED_BYTES
+V_BF_AT = [FREE_AT + (PACK + t) * PICKED_BYTES for t in range(PACK)]
 
 def tile_attend_kernelridge_pl_kernel(tc, query, pts_words, pts_scales, kn, qn, us, coef, offs, out_0, out_1, out_2):
     nc = tc.nc
@@ -77,39 +85,43 @@ def tile_attend_kernelridge_pl_kernel(tc, query, pts_words, pts_scales, kn, qn, 
 
         scale_rows = sb.tile([P, I], U8, name="scale_rows", align_bytes=64)
         nc.vector.tensor_copy(scale_rows[:], scales_all[:].indirect(offsets[:]))
-        for row in range(4):
-            nc.sync.dma_start(scales[row::32, :].bitcast(I32), scale_rows[P - ROWS + row :: 4, :].bitcast(I32))
+        for row in range(LIVE):
+            nc.sync.dma_start(
+                scales[row :: P // QUADRANTS, :].bitcast(I32), scale_rows[P - ROWS + row :: LIVE, :].bitcast(I32)
+            )
         nc.sync.dma_start(coef_all[1][:], coef_planes[:, 1, :])
+
+        words = sb.tile([P, I], U16, name="words", align_bytes=64)
+        nc.vector.tensor_copy(words[:], words_all[:].indirect(offsets[:]))
+        us_col = shared.tile([P, PACK], F32, name="us_col", align_bytes=64, offset=US_AT)
+        nc.sync.dma_start(us_col[:], us.rearrange("o (p t) -> p (o t)", t=PACK))
+        nc.sync.dma_start(coef_all[2][:], coef_planes[:, 2, :])
 
         kn_row = shared.tile([P, I], F32, name="kn_row", align_bytes=64, offset=KN_ROW_AT)
         nc.vector.tensor_copy(
             kn_row[:].bitcast(U32).rearrange("r (t p) -> r p t", t=PACK), kn_all[:].bitcast(U32).indirect(offsets[:])
         )
-        us_col = shared.tile([P, PACK], F32, name="us_col", align_bytes=64, offset=KN_AT + 6 * I)
-        nc.sync.dma_start(us_col[:], us.rearrange("o (p t) -> p (o t)", t=PACK))
-        nc.sync.dma_start(coef_all[2][:], coef_planes[:, 2, :])
+        nc.sync.dma_start(coef_all[3][:], coef_planes[:, 3, :])
+
         query_bf = shared.tile([P, Q, PACK], BF16, name="query_bf", align_bytes=64, offset=QUERY_AT)
         nc.scalar.copy(
             query_bf[:].rearrange("p (c i) j -> p c j i", i=RUN),
             query_raw[:].rearrange("p j (c i) -> p c j i", i=RUN),
         )
-        kn_turned = ps.tile([P, PACK, P], F32, name="kn_turned")
-        neg_kn = shared.tile([P, PACK], F32, name="neg_kn", align_bytes=64, offset=RAW_AT + 4 * I)
+
+        qn_turned = ps.tile([P, P], F32, name="qn_turned", tag="columns")
+        nc.tensor.transpose(qn_turned[:], qn_rows[:], ident[:])
+        qn_col = shared.tile([P, HALVES], F32, name="qn_col", align_bytes=64, offset=QN_COL_AT)
+        nc.scalar.copy(qn_col[:], qn_turned[:, P - HALVES :])
+
+        kn_turned = ps.tile([P, PACK, P], F32, name="kn_turned", tag="columns")
+        neg_kn = shared.tile([P, PACK], F32, name="neg_kn", align_bytes=64, offset=NEG_KN_AT)
         for t in range(PACK):
             nc.tensor.transpose(kn_turned[:, t, :], kn_row[:, t * P : (t + 1) * P], ident[:])
         nc.scalar.activation(neg_kn[:], kn_turned[:, :, P - 1], ACT.Copy, scale=-1.0)
 
-        qn_turned = ps.tile([P, P], F32, name="qn_turned")
-        nc.tensor.transpose(qn_turned[:], qn_rows[:], ident[:])
-        qn_col = shared.tile([P, HALVES], F32, name="qn_col", align_bytes=64, offset=RAW_AT + 5 * I)
-        nc.scalar.copy(qn_col[:], qn_turned[:, P - HALVES :])
-
-        words = shared.tile([P, I], U16, name="words", align_bytes=64, offset=KN_AT)
-        nc.vector.tensor_copy(words[:], words_all[:].indirect(offsets[:]))
-        nc.sync.dma_start(coef_all[3][:], coef_planes[:, 3, :])
-
-        query_codes = shared.tile([P, Q], U32, name="query_codes", align_bytes=64, offset=KN_AT + 4 * I)
-        query_scales = shared.tile([P, Q], U8, name="query_scales", align_bytes=64, offset=QN_AT + Q)
+        query_codes = shared.tile([P, Q], U32, name="query_codes", align_bytes=64, offset=QUERY_CODES_AT)
+        query_scales = shared.tile([P, Q], U8, name="query_scales", align_bytes=64, offset=QUERY_SCALES_AT)
         nc.vector.quantize_mx(query_codes[:].bitcast(FP8X4), query_scales[:], query_bf[:].rearrange("p q j -> p (q j)"))
 
         dots = []
@@ -121,32 +133,31 @@ def tile_attend_kernelridge_pl_kernel(tc, query, pts_words, pts_scales, kn, qn, 
                 rhs=words[:].bitcast(FP4X4), rhs_scale=scales[:], start=True, stop=True,
             )
 
-        picked_at = [QN_AT + Q - 2 * I, COEF_AT[0], KERN_AT, KERN_AT + 2 * I]
-        v_bf_at = [VBF_AT + (8 + 2 * t) * I for t in range(PACK)]
-        v_codes_at = [COEF_AT[1], COEF_AT[1] + I, COEF_AT[3], VBF_AT + 4 * I]
-        banks = ["wide0", "turn1", "turn0", "turn3"]
         picked, turned, v_bf, v_codes, v_scales = {}, {}, {}, {}, {}
 
         def gather(t):
-            picked[t] = shared.tile([P, I], BF16, name=f"picked{t}", align_bytes=64, offset=picked_at[t])
+            picked[t] = shared.tile([P, I], BF16, name=f"picked{t}", align_bytes=64, offset=PICKED_AT[t])
             nc.vector.tensor_copy(picked[t][:], coef_all[t][:].indirect(offsets[:]))
 
         def turn(t):
             pairs = picked[t][:].bitcast(F32)
-            turned[t] = ps.tile([P, 2, P], F32, name=f"turned{t}", tag=banks[t])
+            turned[t] = ps.tile([P, 2, P], F32, name=f"turned{t}", tag=f"turn{t}")
             for u in range(2):
                 nc.tensor.transpose(turned[t][:, u, :], pairs[:, u::2], ident[:])
 
         def empty(t):
-            v_bf[t] = shared.tile([P, P * PACK], BF16, name=f"v_bf{t}", align_bytes=64, offset=v_bf_at[t])
-            nc.scalar.copy(v_bf[t][:].bitcast(F32).rearrange("p (m u) -> p m u", u=2), turned[t][:].rearrange("p u m -> p m u"))
+            v_bf[t] = shared.tile([P, P * PACK], BF16, name=f"v_bf{t}", align_bytes=64, offset=V_BF_AT[t])
+            nc.scalar.copy(
+                v_bf[t][:].bitcast(F32).rearrange("p (m u) -> p m u", u=2), turned[t][:].rearrange("p u m -> p m u")
+            )
 
         def quantise(t):
-            v_codes[t] = shared.tile([P, P], U32, name=f"v_codes{t}", align_bytes=64, offset=v_codes_at[t])
+            v_codes[t] = shared.tile([P, P], U32, name=f"v_codes{t}", align_bytes=64, offset=V_CODES_AT[t])
             v_scales[t] = sb.tile([P, P], U8, name=f"v_scales{t}", align_bytes=64)
             nc.vector.quantize_mx(v_codes[t][:].bitcast(FP8X4), v_scales[t][:], v_bf[t][:])
 
         gather(0)
+
         gap = []
         for h in range(HALVES):
             gap_h = sb.tile([P, PACK, P], F32, name=f"gap{h}")
@@ -163,17 +174,19 @@ def tile_attend_kernelridge_pl_kernel(tc, query, pts_words, pts_scales, kn, qn, 
         for h in range(HALVES):
             for t in range(PACK):
                 nc.tensor.transpose(gap_turned[t // 2][:, t % 2, h * P : (h + 1) * P], gap[h][:, t, :], ident[:])
-            if h == 0:
-                turn(0)
-        empty(0)
+
         kern = shared.tile([P, PACK, Q], F32, name="kern", align_bytes=64, offset=KERN_AT)
         for t in range(PACK):
-            nc.scalar.activation(kern[:, t, :], gap_turned[t // 2][:, t % 2, :], ACT.Exp, bias=neg_kn[:, t : t + 1], scale=-1.0)
+            nc.scalar.activation(
+                kern[:, t, :], gap_turned[t // 2][:, t % 2, :], ACT.Exp, bias=neg_kn[:, t : t + 1], scale=-1.0
+            )
 
         gather(1)
-        turn(1)
-        empty(1)
-        w_bf = shared.tile([P, Q, PACK], BF16, name="w_bf", align_bytes=64, offset=COEF_AT[1] + 2 * I)
+        for t in range(2):
+            turn(t)
+            empty(t)
+
+        w_bf = shared.tile([P, Q, PACK], BF16, name="w_bf", align_bytes=64, offset=W_AT)
         nc.vector.tensor_tensor(
             w_bf[:].rearrange("p (c i) t -> p c t i", i=RUN),
             kern[:].rearrange("p t (c i) -> p c t i", i=RUN),
@@ -208,12 +221,14 @@ def tile_attend_kernelridge_pl_kernel(tc, query, pts_words, pts_scales, kn, qn, 
         for h in range(HALVES):
             nc.scalar.copy(result[0][:, :, h * P : (h + 1) * P], sums[h][:, :2, :])
         nc.sync.dma_start(out_planes[:, :2, :], result[0][:])
+
         turn(3)
         empty(3)
         quantise(2)
         product(2)
         quantise(3)
         product(3)
+
         out_bf = sb.tile([P, Q, PACK], BF16, name="out_bf", align_bytes=64)
         for h, copy in enumerate([nc.vector.tensor_copy, nc.scalar.copy]):
             cols = slice(h * P, (h + 1) * P)
@@ -226,7 +241,8 @@ def tile_attend_kernelridge_pl_kernel(tc, query, pts_words, pts_scales, kn, qn, 
         nc.sync.dma_start(out_1[0].rearrange("p q r -> p (q r)").bitcast(I32), out_codes[:].bitcast(I32))
         for quad in range(QUADRANTS):
             queue = nc.sync if quad % 2 else nc.scalar
+            first = quad * (P // QUADRANTS)
             queue.dma_start(
-                out_2[0, 4 * quad : 4 * quad + 4, :].bitcast(I32),
-                out_scales[32 * quad : 32 * quad + 4, :].bitcast(I32),
+                out_2[0, LIVE * quad : LIVE * (quad + 1), :].bitcast(I32),
+                out_scales[first : first + LIVE, :].bitcast(I32),
             )

@@ -28,8 +28,8 @@ PICKED_BYTES = 2 * I
 KN_AT = 0
 KN_ROW_AT = 2 * ROW_BYTES
 SCALES_AT = KN_ROW_AT + 2 * I
-COEF_AT = [8 * ROW_BYTES, KN_ROW_AT + 4 * I, 4 * ROW_BYTES, KN_AT + ROW_BYTES // 2]
-WORDS_AT = COEF_AT[2] - T
+COEF_AT = [8 * ROW_BYTES, 4 * ROW_BYTES, KN_AT + ROW_BYTES // 2, 12 * ROW_BYTES + Q]
+WORDS_AT = COEF_AT[1] - T
 QUERY_CODES_AT = KN_AT + 4 * I
 US_AT = WORDS_AT
 RAW_AT = 6 * ROW_BYTES
@@ -39,10 +39,10 @@ QN_AT = RAW_AT + 4 * PACK * Q
 QUERY_SCALES_AT = QN_AT + Q
 KERN_AT = QN_AT + 4 * P + P
 FREE_AT = 9 * ROW_BYTES
-QUERY_AT = 11 * ROW_BYTES
-PICKED_AT = [QUERY_SCALES_AT - PICKED_BYTES, COEF_AT[0], KERN_AT, KERN_AT + PICKED_BYTES]
-V_CODES_AT = [COEF_AT[1], COEF_AT[1] + 4 * P, COEF_AT[3], FREE_AT + 2 * PICKED_BYTES]
-W_AT = COEF_AT[1] + PICKED_BYTES
+QUERY_AT = 12 * ROW_BYTES
+PICKED_AT = [QUERY_SCALES_AT - PICKED_BYTES, COEF_AT[0], RAW_AT + 3 * I, FREE_AT]
+V_CODES_AT = [FREE_AT + 3 * PICKED_BYTES, FREE_AT + 3 * PICKED_BYTES + 4 * P, COEF_AT[3] + ROW_BYTES // 2, FREE_AT + 2 * PICKED_BYTES]
+W_AT = FREE_AT + 8 * PICKED_BYTES
 V_BF_AT = [FREE_AT + (PACK + t) * PICKED_BYTES for t in range(PACK)]
 
 def tile_attend_kernelridge_pl_kernel(tc, query, pts_words, pts_scales, kn, qn, us, coef, offs, out_0, out_1, out_2):
@@ -78,7 +78,7 @@ def tile_attend_kernelridge_pl_kernel(tc, query, pts_words, pts_scales, kn, qn, 
             out=ident[:], in_=zeros[:], compare_op=mybir.AluOpType.not_equal, fill=1.0,
             base=0, pattern=[[-1, P]], channel_multiplier=1,
         )
-        nc.gpsimd.memset(qn_rows[: P - HALVES, :], 0.0)
+        nc.scalar.copy(qn_rows[: P - HALVES, :], zeros[: P - HALVES, :])
         nc.vector.memset(scales_all[: P - ROWS, :].bitcast(I32), 0)
         nc.vector.memset(kn_all[: P - 1, T // 2 :].bitcast(I32), 0)
         nc.vector.memset(scales[:].bitcast(I32), 0)
@@ -86,22 +86,21 @@ def tile_attend_kernelridge_pl_kernel(tc, query, pts_words, pts_scales, kn, qn, 
         scale_rows = sb.tile([P, I], U8, name="scale_rows", align_bytes=64)
         nc.vector.tensor_copy(scale_rows[:], scales_all[:].indirect(offsets[:]))
         for row in range(LIVE):
-            nc.sync.dma_start(
+            nc.scalar.dma_start(
                 scales[row :: P // QUADRANTS, :].bitcast(I32), scale_rows[P - ROWS + row :: LIVE, :].bitcast(I32)
             )
-        nc.sync.dma_start(coef_all[1][:], coef_planes[:, 1, :])
 
         words = sb.tile([P, I], U16, name="words", align_bytes=64)
         nc.vector.tensor_copy(words[:], words_all[:].indirect(offsets[:]))
         us_col = shared.tile([P, PACK], F32, name="us_col", align_bytes=64, offset=US_AT)
+        nc.sync.dma_start(coef_all[1][:], coef_planes[:, 1, :])
         nc.sync.dma_start(us_col[:], us.rearrange("o (p t) -> p (o t)", t=PACK))
-        nc.sync.dma_start(coef_all[2][:], coef_planes[:, 2, :])
 
         kn_row = shared.tile([P, I], F32, name="kn_row", align_bytes=64, offset=KN_ROW_AT)
         nc.vector.tensor_copy(
             kn_row[:].bitcast(U32).rearrange("r (t p) -> r p t", t=PACK), kn_all[:].bitcast(U32).indirect(offsets[:])
         )
-        nc.sync.dma_start(coef_all[3][:], coef_planes[:, 3, :])
+        nc.sync.dma_start(coef_all[2][:], coef_planes[:, 2, :])
 
         query_bf = shared.tile([P, Q, PACK], BF16, name="query_bf", align_bytes=64, offset=QUERY_AT)
         nc.scalar.copy(
@@ -123,6 +122,7 @@ def tile_attend_kernelridge_pl_kernel(tc, query, pts_words, pts_scales, kn, qn, 
         query_codes = shared.tile([P, Q], U32, name="query_codes", align_bytes=64, offset=QUERY_CODES_AT)
         query_scales = shared.tile([P, Q], U8, name="query_scales", align_bytes=64, offset=QUERY_SCALES_AT)
         nc.vector.quantize_mx(query_codes[:].bitcast(FP8X4), query_scales[:], query_bf[:].rearrange("p q j -> p (q j)"))
+        nc.sync.dma_start(coef_all[3][:], coef_planes[:, 3, :])
 
         dots = []
         for h in range(HALVES):
@@ -170,35 +170,38 @@ def tile_attend_kernelridge_pl_kernel(tc, query, pts_words, pts_scales, kn, qn, 
             )
             gap.append(gap_h)
 
-        gap_turned = [ps.tile([P, 2, Q], F32, name=f"gap_turned{u}", tag=f"turn{u}") for u in range(PACK // 2)]
+        kern = []
         for h in range(HALVES):
+            gap_turned = ps.tile([P, PACK, P], F32, name=f"gap_turned{h}", tag=f"turn{h}")
             for t in range(PACK):
-                nc.tensor.transpose(gap_turned[t // 2][:, t % 2, h * P : (h + 1) * P], gap[h][:, t, :], ident[:])
-
-        kern = shared.tile([P, PACK, Q], F32, name="kern", align_bytes=64, offset=KERN_AT)
-        for t in range(PACK):
-            nc.scalar.activation(
-                kern[:, t, :], gap_turned[t // 2][:, t % 2, :], ACT.Exp, bias=neg_kn[:, t : t + 1], scale=-1.0
-            )
+                nc.tensor.transpose(gap_turned[:, t, :], gap[h][:, t, :], ident[:])
+            kern.append(sb.tile([P, PACK, P], F32, name=f"kern{h}"))
+            for t in range(PACK):
+                nc.scalar.activation(
+                    kern[h][:, t, :], gap_turned[:, t, :], ACT.Exp, bias=neg_kn[:, t : t + 1], scale=-1.0
+                )
 
         gather(1)
         for t in range(2):
             turn(t)
             empty(t)
 
-        w_bf = shared.tile([P, Q, PACK], BF16, name="w_bf", align_bytes=64, offset=W_AT)
-        nc.vector.tensor_tensor(
-            w_bf[:].rearrange("p (c i) t -> p c t i", i=RUN),
-            kern[:].rearrange("p t (c i) -> p c t i", i=RUN),
-            us_col[:].unsqueeze(1).unsqueeze(3).to_broadcast([P, Q // RUN, PACK, RUN]),
-            mybir.AluOpType.mult,
-        )
+        w_bf = []
+        for h in range(HALVES):
+            w_bf.append(sb.tile([P, P, PACK], BF16, name=f"w_bf{h}", align_bytes=64))
+            nc.vector.tensor_tensor(
+                w_bf[h][:].rearrange("p (c i) t -> p c t i", i=RUN),
+                kern[h][:].rearrange("p t (c i) -> p c t i", i=RUN),
+                us_col[:].unsqueeze(1).unsqueeze(3).to_broadcast([P, P // RUN, PACK, RUN]),
+                mybir.AluOpType.mult,
+            )
+        gather(2)
+        w_codes = [sb.tile([P, P], U32, name=f"w_codes{h}", align_bytes=64) for h in range(HALVES)]
+        w_scales = [sb.tile([P, P], U8, name=f"w_scales{h}", align_bytes=64) for h in range(HALVES)]
+        for h in range(HALVES):
+            nc.vector.quantize_mx(w_codes[h][:].bitcast(FP8X4), w_scales[h][:], w_bf[h][:].rearrange("p q t -> p (q t)"))
         quantise(0)
         quantise(1)
-        w_codes = sb.tile([P, Q], U32, name="w_codes", align_bytes=64)
-        w_scales = sb.tile([P, Q], U8, name="w_scales", align_bytes=64)
-        nc.vector.quantize_mx(w_codes[:].bitcast(FP8X4), w_scales[:], w_bf[:].rearrange("p q t -> p (q t)"))
-        gather(2)
         turn(2)
         empty(2)
         gather(3)
@@ -207,10 +210,9 @@ def tile_attend_kernelridge_pl_kernel(tc, query, pts_words, pts_scales, kn, qn, 
 
         def product(t):
             for h in range(HALVES):
-                cols = slice(h * P, (h + 1) * P)
                 nc.tensor.matmul_mx(
                     sums[h][:, t, :], lhsT=v_codes[t][:].bitcast(FP8X4), lhsT_scale=v_scales[t][:],
-                    rhs=w_codes[:, cols].bitcast(FP8X4), rhs_scale=w_scales[:, cols], start=True, stop=True,
+                    rhs=w_codes[h][:].bitcast(FP8X4), rhs_scale=w_scales[h][:], start=True, stop=True,
                 )
 
         out_planes = out_0.rearrange("(p t) q -> p t q", t=PACK)

@@ -54,40 +54,42 @@ def tile_attend_kernelridge_pl_kernel(tc, query, pts_words, pts_scales, kn, qn, 
 
         offsets = sb.tile([P, I // 16], U16, name="offsets")
         words_all = shared.tile([P, T], U16, name="words_all", align_bytes=64, offset=WORDS_AT)
-        scales_all = shared.tile([P, T], U8, name="scales_all", align_bytes=64, offset=SCALES_AT)
+        scales_all = shared.tile([P, T + 4], U8, name="scales_all", align_bytes=64, offset=SCALES_AT)
         kn_all = shared.tile([P, T], F32, name="kn_all", align_bytes=64, offset=KN_AT)
         query_raw = shared.tile([P, PACK, Q], F32, name="query_raw", align_bytes=64, offset=RAW_AT)
         coef_all = [shared.tile([P, T], F32, name=f"coef_all{t}", align_bytes=64, offset=COEF_AT[t]) for t in range(PACK)]
         qn_rows = shared.tile([P, P], F32, name="qn_rows", align_bytes=64, offset=QN_AT)
         zeros = sb.tile([P, P], F32, name="zeros")
         ident = sb.tile([P, P], F32, name="ident")
-        scales = sb.tile([P, I], U8, name="scales", align_bytes=64)
+        scales = sb.tile([P, I + 4], U8, name="scales", align_bytes=64)
 
         coef_planes = coef.rearrange("(p t) n -> p t n", t=PACK)
         nc.sync.dma_start(offsets[:], offs)
-        nc.sync.dma_start(scales_all[P - ROWS :, :].bitcast(I32), pts_scales[0].bitcast(I32))
+        nc.scalar.dma_start(scales_all[P // 2 - ROWS : P // 2, :T].bitcast(I32), pts_scales[0].bitcast(I32))
         nc.scalar.dma_start(kn_all[P - 1 :, :], kn[0:1, :])
         nc.sync.dma_start(words_all[:].bitcast(I32), pts_words[0].bitcast(I32))
         nc.sync.dma_start(query_raw[:], query.rearrange("(p j) q -> p j q", j=PACK))
-        nc.sync.dma_start(qn_rows[P - HALVES :, :], qn.rearrange("(h p) o -> h (p o)", p=P))
+        nc.scalar.dma_start(qn_rows[P - HALVES :, :], qn.rearrange("(h p) o -> h (p o)", p=P))
         nc.sync.dma_start(coef_all[0][:], coef_planes[:, 0, :])
 
-        nc.gpsimd.memset(kn_all[: P - 1, : T // 2].bitcast(I32), 0)
+        nc.gpsimd.memset(kn_all[: P - 1, : 3 * T // 4].bitcast(I32), 0)
         nc.gpsimd.memset(zeros[:], 0.0)
         nc.gpsimd.affine_select(
             out=ident[:], in_=zeros[:], compare_op=mybir.AluOpType.not_equal, fill=1.0,
             base=0, pattern=[[-1, P]], channel_multiplier=1,
         )
         nc.scalar.copy(qn_rows[: P - HALVES, :], zeros[: P - HALVES, :])
-        nc.vector.memset(scales_all[: P - ROWS, :].bitcast(I32), 0)
-        nc.vector.memset(kn_all[: P - 1, T // 2 :].bitcast(I32), 0)
+        nc.vector.memset(scales_all[: P // 2 - ROWS, :].bitcast(I32), 0)
+        nc.vector.memset(scales_all[P // 2 :, :].bitcast(I32), 0)
         nc.vector.memset(scales[:].bitcast(I32), 0)
+        nc.vector.memset(kn_all[: P - 1, 3 * T // 4 :].bitcast(I32), 0)
 
         scale_rows = sb.tile([P, I], U8, name="scale_rows", align_bytes=64)
-        nc.vector.tensor_copy(scale_rows[:], scales_all[:].indirect(offsets[:]))
+        nc.vector.tensor_copy(scale_rows[:], scales_all[:, :T].indirect(offsets[:]))
         for row in range(LIVE):
             nc.scalar.dma_start(
-                scales[row :: P // QUADRANTS, :].bitcast(I32), scale_rows[P - ROWS + row :: LIVE, :].bitcast(I32)
+                scales[row :: P // QUADRANTS, :I].bitcast(I32),
+                scale_rows[P // 2 - ROWS + row : P // 2 : LIVE, :].bitcast(I32),
             )
 
         words = sb.tile([P, I], U16, name="words", align_bytes=64)
@@ -103,10 +105,12 @@ def tile_attend_kernelridge_pl_kernel(tc, query, pts_words, pts_scales, kn, qn, 
         nc.sync.dma_start(coef_all[2][:], coef_planes[:, 2, :])
 
         query_bf = shared.tile([P, Q, PACK], BF16, name="query_bf", align_bytes=64, offset=QUERY_AT)
-        nc.scalar.copy(
-            query_bf[:].rearrange("p (c i) j -> p c j i", i=RUN),
-            query_raw[:].rearrange("p j (c i) -> p c j i", i=RUN),
-        )
+        for h in range(HALVES):
+            cols = slice(h * P, (h + 1) * P)
+            nc.scalar.copy(
+                query_bf[:, cols, :].rearrange("p (c i) j -> p c j i", i=RUN),
+                query_raw[:, :, cols].rearrange("p j (c i) -> p c j i", i=RUN),
+            )
 
         qn_turned = ps.tile([P, P], F32, name="qn_turned", tag="columns")
         nc.tensor.transpose(qn_turned[:], qn_rows[:], ident[:])
@@ -121,7 +125,11 @@ def tile_attend_kernelridge_pl_kernel(tc, query, pts_words, pts_scales, kn, qn, 
 
         query_codes = shared.tile([P, Q], U32, name="query_codes", align_bytes=64, offset=QUERY_CODES_AT)
         query_scales = shared.tile([P, Q], U8, name="query_scales", align_bytes=64, offset=QUERY_SCALES_AT)
-        nc.vector.quantize_mx(query_codes[:].bitcast(FP8X4), query_scales[:], query_bf[:].rearrange("p q j -> p (q j)"))
+        for h in range(HALVES):
+            cols = slice(h * P, (h + 1) * P)
+            nc.vector.quantize_mx(
+                query_codes[:, cols].bitcast(FP8X4), query_scales[:, cols], query_bf[:, cols, :].rearrange("p q j -> p (q j)")
+            )
         nc.sync.dma_start(coef_all[3][:], coef_planes[:, 3, :])
 
         dots = []
@@ -130,7 +138,7 @@ def tile_attend_kernelridge_pl_kernel(tc, query, pts_words, pts_scales, kn, qn, 
             dots.append(ps.tile([P, I], F32, name=f"dots{h}", tag=f"wide{h}"))
             nc.tensor.matmul_mx(
                 dots[h][:], lhsT=query_codes[:, cols].bitcast(FP8X4), lhsT_scale=query_scales[:, cols],
-                rhs=words[:].bitcast(FP4X4), rhs_scale=scales[:], start=True, stop=True,
+                rhs=words[:].bitcast(FP4X4), rhs_scale=scales[:, :I], start=True, stop=True,
             )
 
         picked, turned, v_bf, v_codes, v_scales = {}, {}, {}, {}, {}
@@ -228,18 +236,24 @@ def tile_attend_kernelridge_pl_kernel(tc, query, pts_words, pts_scales, kn, qn, 
         empty(3)
         quantise(2)
         product(2)
+        for h in range(HALVES):
+            nc.scalar.copy(result[1][:, 0, h * P : (h + 1) * P], sums[h][:, 2, :])
+        nc.sync.dma_start(out_planes[:, 2, :], result[1][:, 0, :])
         quantise(3)
         product(3)
 
-        out_bf = sb.tile([P, Q, PACK], BF16, name="out_bf", align_bytes=64)
+        out_bf = [sb.tile([P, P, PACK], BF16, name=f"out_bf{h}", align_bytes=64) for h in range(HALVES)]
         for h, copy in enumerate([nc.vector.tensor_copy, nc.scalar.copy]):
-            cols = slice(h * P, (h + 1) * P)
-            copy(out_bf[:, cols, :], sums[h][:].rearrange("p t q -> p q t"))
-            copy(result[1][:, :, cols], sums[h][:, 2:, :])
-        nc.scalar.dma_start(out_planes[:, 2:, :], result[1][:])
+            copy(out_bf[h][:], sums[h][:].rearrange("p t q -> p q t"))
+        last = sb.tile([P, Q], F32, name="last")
+        for h in reversed(range(HALVES)):
+            nc.scalar.copy(last[:, h * P : (h + 1) * P], sums[h][:, 3, :])
+        nc.scalar.dma_start(out_planes[:, 3, :], last[:])
         out_codes = sb.tile([P, Q], U32, name="out_codes", align_bytes=64)
         out_scales = sb.tile([P, Q], U8, name="out_scales", align_bytes=64)
-        nc.vector.quantize_mx(out_codes[:].bitcast(FP8X4), out_scales[:], out_bf[:].rearrange("p q t -> p (q t)"))
+        for h in reversed(range(HALVES)):
+            cols = slice(h * P, (h + 1) * P)
+            nc.vector.quantize_mx(out_codes[:, cols].bitcast(FP8X4), out_scales[:, cols], out_bf[h][:].rearrange("p q t -> p (q t)"))
         nc.sync.dma_start(out_1[0].rearrange("p q r -> p (q r)").bitcast(I32), out_codes[:].bitcast(I32))
         for quad in range(QUADRANTS):
             queue = nc.sync if quad % 2 else nc.scalar

@@ -22,28 +22,19 @@ QUADRANTS = 4
 LIVE = 4
 ROWS = QUADRANTS * LIVE
 RUN = 4
+SPARE = 4
 
-ROW_BYTES = 4 * T
-PICKED_BYTES = 2 * I
-KN_AT = 0
-KN_ROW_AT = 2 * ROW_BYTES
-SCALES_AT = KN_ROW_AT + 2 * I
-COEF_AT = [8 * ROW_BYTES, 4 * ROW_BYTES, KN_AT + ROW_BYTES // 2, 12 * ROW_BYTES + Q]
-WORDS_AT = COEF_AT[1] - T
-QUERY_CODES_AT = KN_AT + 4 * I
-US_AT = WORDS_AT
-RAW_AT = 6 * ROW_BYTES
-NEG_KN_AT = RAW_AT + 4 * I
-QN_COL_AT = RAW_AT + 5 * I
-QN_AT = RAW_AT + 4 * PACK * Q
-QUERY_SCALES_AT = QN_AT + Q
-KERN_AT = QN_AT + 4 * P + P
-FREE_AT = 9 * ROW_BYTES
-QUERY_AT = 12 * ROW_BYTES
-PICKED_AT = [QUERY_SCALES_AT - PICKED_BYTES, COEF_AT[0], RAW_AT + 3 * I, FREE_AT]
-V_CODES_AT = [FREE_AT + 3 * PICKED_BYTES, FREE_AT + 3 * PICKED_BYTES + 4 * P, COEF_AT[3] + ROW_BYTES // 2, FREE_AT + 2 * PICKED_BYTES]
-W_AT = FREE_AT + 8 * PICKED_BYTES
-V_BF_AT = [FREE_AT + (PACK + t) * PICKED_BYTES for t in range(PACK)]
+KB = 1024
+SCALES_AT = 0
+KN_AT = 4 * KB
+WORDS_AT = 18 * KB
+RAW_AT = 32 * KB
+QN_AT = RAW_AT + 4 * KB
+QUERY_AT = 40 * KB
+COEF_AT = [52 * KB, WORDS_AT + 2 * KB, KN_AT + 4 * KB, QUERY_AT + KB]
+PICKED_AT = [QN_AT - 3 * KB // 4, COEF_AT[0], RAW_AT + KB + KB // 2, 60 * KB]
+LATE_AT = COEF_AT[3] + 2 * KB
+
 
 def tile_attend_kernelridge_pl_kernel(tc, query, pts_words, pts_scales, kn, qn, us, coef, offs, out_0, out_1, out_2):
     nc = tc.nc
@@ -52,20 +43,29 @@ def tile_attend_kernelridge_pl_kernel(tc, query, pts_words, pts_scales, kn, qn, 
         shared = ctx.enter_context(tc.tile_pool(name="shared", bufs=1))
         ps = ctx.enter_context(tc.psum_pool(name="ps", bufs=1))
 
-        offsets = sb.tile([P, I // 16], U16, name="offsets")
-        words_all = shared.tile([P, T], U16, name="words_all", align_bytes=64, offset=WORDS_AT)
-        scales_all = shared.tile([P, T + 4], U8, name="scales_all", align_bytes=64, offset=SCALES_AT)
-        kn_all = shared.tile([P, T], F32, name="kn_all", align_bytes=64, offset=KN_AT)
-        query_raw = shared.tile([P, PACK, Q], F32, name="query_raw", align_bytes=64, offset=RAW_AT)
-        coef_all = [shared.tile([P, T], F32, name=f"coef_all{t}", align_bytes=64, offset=COEF_AT[t]) for t in range(PACK)]
-        qn_rows = shared.tile([P, P], F32, name="qn_rows", align_bytes=64, offset=QN_AT)
-        zeros = sb.tile([P, P], F32, name="zeros")
-        ident = sb.tile([P, P], F32, name="ident")
-        scales = sb.tile([P, I + 4], U8, name="scales", align_bytes=64)
+        def placed(name, shape, dtype, offset):
+            return shared.tile(shape, dtype, name=name, align_bytes=64, offset=offset)
 
+        def own(name, shape, dtype):
+            return sb.tile(shape, dtype, name=name, align_bytes=64)
+
+        halves = [slice(h * P, (h + 1) * P) for h in range(HALVES)]
+
+        offsets = sb.tile([P, I // 16], U16, name="offsets")
+        words_all = placed("words_all", [P, T], U16, WORDS_AT)
+        scales_all = placed("scales_all", [P, T + SPARE], U8, SCALES_AT)
+        kn_all = placed("kn_all", [P, T], F32, KN_AT)
+        query_raw = placed("query_raw", [P, PACK, Q], F32, RAW_AT)
+        qn_rows = placed("qn_rows", [P, P], F32, QN_AT)
+        coef_all = [placed(f"coef_all{t}", [P, T], F32, COEF_AT[t]) for t in range(PACK)]
+        zeros = own("zeros", [P, P], F32)
+        ident = own("ident", [P, P], F32)
+        scales = own("scales", [P, I + SPARE], U8)
+
+        first_row = P // 2 - ROWS
         coef_planes = coef.rearrange("(p t) n -> p t n", t=PACK)
         nc.sync.dma_start(offsets[:], offs)
-        nc.scalar.dma_start(scales_all[P // 2 - ROWS : P // 2, :T].bitcast(I32), pts_scales[0].bitcast(I32))
+        nc.scalar.dma_start(scales_all[first_row : P // 2, :T].bitcast(I32), pts_scales[0].bitcast(I32))
         nc.scalar.dma_start(kn_all[P - 1 :, :], kn[0:1, :])
         nc.sync.dma_start(words_all[:].bitcast(I32), pts_words[0].bitcast(I32))
         nc.sync.dma_start(query_raw[:], query.rearrange("(p j) q -> p j q", j=PACK))
@@ -79,34 +79,33 @@ def tile_attend_kernelridge_pl_kernel(tc, query, pts_words, pts_scales, kn, qn, 
             base=0, pattern=[[-1, P]], channel_multiplier=1,
         )
         nc.scalar.copy(qn_rows[: P - HALVES, :], zeros[: P - HALVES, :])
-        nc.vector.memset(scales_all[: P // 2 - ROWS, :].bitcast(I32), 0)
+        nc.vector.memset(scales_all[:first_row, :].bitcast(I32), 0)
         nc.vector.memset(scales_all[P // 2 :, :].bitcast(I32), 0)
         nc.vector.memset(scales[:].bitcast(I32), 0)
         nc.vector.memset(kn_all[: P - 1, 3 * T // 4 :].bitcast(I32), 0)
 
-        scale_rows = sb.tile([P, I], U8, name="scale_rows", align_bytes=64)
+        scale_rows = own("scale_rows", [P, I], U8)
         nc.vector.tensor_copy(scale_rows[:], scales_all[:, :T].indirect(offsets[:]))
         for row in range(LIVE):
             nc.scalar.dma_start(
                 scales[row :: P // QUADRANTS, :I].bitcast(I32),
-                scale_rows[P // 2 - ROWS + row : P // 2 : LIVE, :].bitcast(I32),
+                scale_rows[first_row + row : P // 2 : LIVE, :].bitcast(I32),
             )
 
-        words = sb.tile([P, I], U16, name="words", align_bytes=64)
+        words = own("words", [P, I], U16)
         nc.vector.tensor_copy(words[:], words_all[:].indirect(offsets[:]))
-        us_col = shared.tile([P, PACK], F32, name="us_col", align_bytes=64, offset=US_AT)
+        us_col = placed("us_col", [P, PACK], F32, WORDS_AT)
         nc.sync.dma_start(coef_all[1][:], coef_planes[:, 1, :])
         nc.sync.dma_start(us_col[:], us.rearrange("o (p t) -> p (o t)", t=PACK))
 
-        kn_row = shared.tile([P, I], F32, name="kn_row", align_bytes=64, offset=KN_ROW_AT)
+        kn_row = placed("kn_row", [P, I], F32, SCALES_AT)
         nc.vector.tensor_copy(
             kn_row[:].bitcast(U32).rearrange("r (t p) -> r p t", t=PACK), kn_all[:].bitcast(U32).indirect(offsets[:])
         )
         nc.sync.dma_start(coef_all[2][:], coef_planes[:, 2, :])
 
-        query_bf = shared.tile([P, Q, PACK], BF16, name="query_bf", align_bytes=64, offset=QUERY_AT)
-        for h in range(HALVES):
-            cols = slice(h * P, (h + 1) * P)
+        query_bf = placed("query_bf", [P, Q, PACK], BF16, QUERY_AT)
+        for cols in halves:
             nc.scalar.copy(
                 query_bf[:, cols, :].rearrange("p (c i) j -> p c j i", i=RUN),
                 query_raw[:, :, cols].rearrange("p j (c i) -> p c j i", i=RUN),
@@ -114,27 +113,26 @@ def tile_attend_kernelridge_pl_kernel(tc, query, pts_words, pts_scales, kn, qn, 
 
         qn_turned = ps.tile([P, P], F32, name="qn_turned", tag="columns")
         nc.tensor.transpose(qn_turned[:], qn_rows[:], ident[:])
-        qn_col = shared.tile([P, HALVES], F32, name="qn_col", align_bytes=64, offset=QN_COL_AT)
+        qn_col = placed("qn_col", [P, HALVES], F32, RAW_AT + 2 * KB + KB // 2)
         nc.scalar.copy(qn_col[:], qn_turned[:, P - HALVES :])
 
         kn_turned = ps.tile([P, PACK, P], F32, name="kn_turned", tag="columns")
-        neg_kn = shared.tile([P, PACK], F32, name="neg_kn", align_bytes=64, offset=NEG_KN_AT)
+        neg_kn = placed("neg_kn", [P, PACK], F32, RAW_AT + 2 * KB)
         for t in range(PACK):
             nc.tensor.transpose(kn_turned[:, t, :], kn_row[:, t * P : (t + 1) * P], ident[:])
         nc.scalar.activation(neg_kn[:], kn_turned[:, :, P - 1], ACT.Copy, scale=-1.0)
 
-        query_codes = shared.tile([P, Q], U32, name="query_codes", align_bytes=64, offset=QUERY_CODES_AT)
-        query_scales = shared.tile([P, Q], U8, name="query_scales", align_bytes=64, offset=QUERY_SCALES_AT)
-        for h in range(HALVES):
-            cols = slice(h * P, (h + 1) * P)
+        query_codes = placed("query_codes", [P, Q], U32, KN_AT + 2 * KB)
+        query_scales = placed("query_scales", [P, Q], U8, QN_AT + KB // 4)
+        for cols in halves:
             nc.vector.quantize_mx(
-                query_codes[:, cols].bitcast(FP8X4), query_scales[:, cols], query_bf[:, cols, :].rearrange("p q j -> p (q j)")
+                query_codes[:, cols].bitcast(FP8X4), query_scales[:, cols],
+                query_bf[:, cols, :].rearrange("p q j -> p (q j)"),
             )
         nc.sync.dma_start(coef_all[3][:], coef_planes[:, 3, :])
 
         dots = []
-        for h in range(HALVES):
-            cols = slice(h * P, (h + 1) * P)
+        for h, cols in enumerate(halves):
             dots.append(ps.tile([P, I], F32, name=f"dots{h}", tag=f"wide{h}"))
             nc.tensor.matmul_mx(
                 dots[h][:], lhsT=query_codes[:, cols].bitcast(FP8X4), lhsT_scale=query_scales[:, cols],
@@ -144,7 +142,7 @@ def tile_attend_kernelridge_pl_kernel(tc, query, pts_words, pts_scales, kn, qn, 
         picked, turned, v_bf, v_codes, v_scales = {}, {}, {}, {}, {}
 
         def gather(t):
-            picked[t] = shared.tile([P, I], BF16, name=f"picked{t}", align_bytes=64, offset=PICKED_AT[t])
+            picked[t] = placed(f"picked{t}", [P, I], BF16, PICKED_AT[t])
             nc.vector.tensor_copy(picked[t][:], coef_all[t][:].indirect(offsets[:]))
 
         def turn(t):
@@ -154,36 +152,33 @@ def tile_attend_kernelridge_pl_kernel(tc, query, pts_words, pts_scales, kn, qn, 
                 nc.tensor.transpose(turned[t][:, u, :], pairs[:, u::2], ident[:])
 
         def empty(t):
-            v_bf[t] = shared.tile([P, P * PACK], BF16, name=f"v_bf{t}", align_bytes=64, offset=V_BF_AT[t])
+            v_bf[t] = own(f"v_bf{t}", [P, P * PACK], BF16)
             nc.scalar.copy(
                 v_bf[t][:].bitcast(F32).rearrange("p (m u) -> p m u", u=2), turned[t][:].rearrange("p u m -> p m u")
             )
 
         def quantise(t):
-            v_codes[t] = shared.tile([P, P], U32, name=f"v_codes{t}", align_bytes=64, offset=V_CODES_AT[t])
-            v_scales[t] = sb.tile([P, P], U8, name=f"v_scales{t}", align_bytes=64)
+            v_codes[t] = placed("v_codes2", [P, P], U32, LATE_AT) if t == 2 else own(f"v_codes{t}", [P, P], U32)
+            v_scales[t] = own(f"v_scales{t}", [P, P], U8)
             nc.vector.quantize_mx(v_codes[t][:].bitcast(FP8X4), v_scales[t][:], v_bf[t][:])
 
         gather(0)
 
         gap = []
         for h in range(HALVES):
-            gap_h = sb.tile([P, PACK, P], F32, name=f"gap{h}")
+            gap.append(own(f"gap{h}", [P, PACK, P], F32))
             nc.scalar.activation(
-                gap_h[:].rearrange("q t (c i) -> q c t i", i=RUN),
+                gap[h][:].rearrange("q t (c i) -> q c t i", i=RUN),
                 dots[h][:].rearrange("q (c i t) -> q c t i", i=RUN, t=PACK),
-                ACT.Identity,
-                bias=qn_col[:, h : h + 1],
-                scale=-1.0,
+                ACT.Identity, bias=qn_col[:, h : h + 1], scale=-1.0,
             )
-            gap.append(gap_h)
 
         kern = []
         for h in range(HALVES):
             gap_turned = ps.tile([P, PACK, P], F32, name=f"gap_turned{h}", tag=f"turn{h}")
             for t in range(PACK):
                 nc.tensor.transpose(gap_turned[:, t, :], gap[h][:, t, :], ident[:])
-            kern.append(sb.tile([P, PACK, P], F32, name=f"kern{h}"))
+            kern.append(own(f"kern{h}", [P, PACK, P], F32))
             for t in range(PACK):
                 nc.scalar.activation(
                     kern[h][:, t, :], gap_turned[:, t, :], ACT.Exp, bias=neg_kn[:, t : t + 1], scale=-1.0
@@ -196,7 +191,7 @@ def tile_attend_kernelridge_pl_kernel(tc, query, pts_words, pts_scales, kn, qn, 
 
         w_bf = []
         for h in range(HALVES):
-            w_bf.append(sb.tile([P, P, PACK], BF16, name=f"w_bf{h}", align_bytes=64))
+            w_bf.append(own(f"w_bf{h}", [P, P, PACK], BF16))
             nc.vector.tensor_tensor(
                 w_bf[h][:].rearrange("p (c i) t -> p c t i", i=RUN),
                 kern[h][:].rearrange("p t (c i) -> p c t i", i=RUN),
@@ -204,56 +199,61 @@ def tile_attend_kernelridge_pl_kernel(tc, query, pts_words, pts_scales, kn, qn, 
                 mybir.AluOpType.mult,
             )
         gather(2)
-        w_codes = [sb.tile([P, P], U32, name=f"w_codes{h}", align_bytes=64) for h in range(HALVES)]
-        w_scales = [sb.tile([P, P], U8, name=f"w_scales{h}", align_bytes=64) for h in range(HALVES)]
-        for h in range(HALVES):
-            nc.vector.quantize_mx(w_codes[h][:].bitcast(FP8X4), w_scales[h][:], w_bf[h][:].rearrange("p q t -> p (q t)"))
+        w_codes = own("w_codes", [P, Q], U32)
+        w_scales = own("w_scales", [P, Q], U8)
+        for h, cols in enumerate(halves):
+            nc.vector.quantize_mx(
+                w_codes[:, cols].bitcast(FP8X4), w_scales[:, cols], w_bf[h][:].rearrange("p q t -> p (q t)")
+            )
         quantise(0)
         quantise(1)
         turn(2)
         empty(2)
         gather(3)
 
-        sums = [ps.tile([P, PACK, P], F32, name=f"sums{h}", tag=f"wide{h}") for h in range(HALVES)]
-
-        def product(t):
-            for h in range(HALVES):
-                nc.tensor.matmul_mx(
-                    sums[h][:, t, :], lhsT=v_codes[t][:].bitcast(FP8X4), lhsT_scale=v_scales[t][:],
-                    rhs=w_codes[h][:].bitcast(FP8X4), rhs_scale=w_scales[h][:], start=True, stop=True,
-                )
+        def product(out, t, cols):
+            nc.tensor.matmul_mx(
+                out, lhsT=v_codes[t][:].bitcast(FP8X4), lhsT_scale=v_scales[t][:],
+                rhs=w_codes[:, cols].bitcast(FP8X4), rhs_scale=w_scales[:, cols], start=True, stop=True,
+            )
 
         out_planes = out_0.rearrange("(p t) q -> p t q", t=PACK)
+        out_bf = placed("out_bf", [P, Q, PACK], BF16, LATE_AT + KB)
+        early = [ps.tile([P, 2, P], F32, name=f"early{h}", tag=f"wide{h}") for h in range(HALVES)]
+        result_early = own("result_early", [P, 2, Q], F32)
+        for t in range(2):
+            for h, cols in enumerate(halves):
+                product(early[h][:, t, :], t, cols)
+        for h, cols in enumerate(halves):
+            nc.scalar.copy(result_early[:, :, cols], early[h][:])
+        nc.sync.dma_start(out_planes[:, :2, :], result_early[:])
 
-        result = [sb.tile([P, 2, Q], F32, name=f"result{u}") for u in range(2)]
-        product(0)
-        product(1)
-        for h in range(HALVES):
-            nc.scalar.copy(result[0][:, :, h * P : (h + 1) * P], sums[h][:, :2, :])
-        nc.sync.dma_start(out_planes[:, :2, :], result[0][:])
-
+        copies = [nc.vector.tensor_copy, nc.scalar.copy]
+        quantise(2)
+        for h in reversed(range(HALVES)):
+            copies[h](out_bf[:, halves[h], :2], early[h][:].rearrange("p t q -> p q t"))
         turn(3)
         empty(3)
-        quantise(2)
-        product(2)
-        for h in range(HALVES):
-            nc.scalar.copy(result[1][:, 0, h * P : (h + 1) * P], sums[h][:, 2, :])
-        nc.sync.dma_start(out_planes[:, 2, :], result[1][:, 0, :])
+        late = [ps.tile([P, 2, P], F32, name=f"late{h}", tag=f"turn{h}") for h in range(HALVES)]
+        third = ps.tile([P, Q], F32, name="third", tag="turn2")
+        product(third[:], 2, slice(0, Q))
+        for h, cols in enumerate(halves):
+            product(late[h][:, 0, :], 2, cols)
+        result_third = own("result_third", [P, Q], F32)
+        nc.scalar.copy(result_third[:], third[:])
+        nc.sync.dma_start(out_planes[:, 2, :], result_third[:])
         quantise(3)
-        product(3)
+        for h, cols in enumerate(halves):
+            product(late[h][:, 1, :], 3, cols)
 
-        out_bf = [sb.tile([P, P, PACK], BF16, name=f"out_bf{h}", align_bytes=64) for h in range(HALVES)]
-        for h, copy in enumerate([nc.vector.tensor_copy, nc.scalar.copy]):
-            copy(out_bf[h][:], sums[h][:].rearrange("p t q -> p q t"))
-        last = sb.tile([P, Q], F32, name="last")
-        for h in reversed(range(HALVES)):
-            nc.scalar.copy(last[:, h * P : (h + 1) * P], sums[h][:, 3, :])
-        nc.scalar.dma_start(out_planes[:, 3, :], last[:])
-        out_codes = sb.tile([P, Q], U32, name="out_codes", align_bytes=64)
-        out_scales = sb.tile([P, Q], U8, name="out_scales", align_bytes=64)
-        for h in reversed(range(HALVES)):
-            cols = slice(h * P, (h + 1) * P)
-            nc.vector.quantize_mx(out_codes[:, cols].bitcast(FP8X4), out_scales[:, cols], out_bf[h][:].rearrange("p q t -> p (q t)"))
+        result_last = own("result_last", [P, Q], F32)
+        for h, copy in enumerate(copies):
+            copy(out_bf[:, halves[h], 2:], late[h][:].rearrange("p t q -> p q t"))
+            copy(result_last[:, halves[h]], late[h][:, 1, :])
+        nc.scalar.dma_start(out_planes[:, 3, :], result_last[:])
+        out_codes = own("out_codes", [P, Q], U32)
+        out_scales = own("out_scales", [P, Q], U8)
+        nc.vector.quantize_mx(out_codes[:].bitcast(FP8X4), out_scales[:], out_bf[:].rearrange("p q t -> p (q t)"))
         nc.sync.dma_start(out_1[0].rearrange("p q r -> p (q r)").bitcast(I32), out_codes[:].bitcast(I32))
         for quad in range(QUADRANTS):
             queue = nc.sync if quad % 2 else nc.scalar

@@ -235,22 +235,17 @@ def tile_attend_kernelridge_pl_kernel(tc, query, pts_words, pts_scales, kn, qn, 
         turn(3)
         empty(3)
         late = [ps.tile([P, 2, P], F32, name=f"late{h}", tag=f"turn{h}") for h in range(HALVES)]
-        third = ps.tile([P, Q], F32, name="third", tag="turn2")
-        product(third[:], 2, slice(0, Q))
         for h, cols in enumerate(halves):
             product(late[h][:, 0, :], 2, cols)
-        result_third = own("result_third", [P, Q], F32)
-        nc.scalar.copy(result_third[:], third[:])
-        nc.sync.dma_start(out_planes[:, 2, :], result_third[:])
         quantise(3)
         for h, cols in enumerate(halves):
             product(late[h][:, 1, :], 3, cols)
 
-        result_last = own("result_last", [P, Q], F32)
+        result_late = own("result_late", [P, 2, Q], F32)
         for h, copy in enumerate(copies):
             copy(out_bf[:, halves[h], 2:], late[h][:].rearrange("p t q -> p q t"))
-            copy(result_last[:, halves[h]], late[h][:, 1, :])
-        nc.scalar.dma_start(out_planes[:, 3, :], result_last[:])
+            copy(result_late[:, :, halves[h]], late[h][:])
+        nc.scalar.dma_start(out_planes[:, 2:, :], result_late[:])
         out_codes = own("out_codes", [P, Q], U32)
         out_scales = own("out_scales", [P, Q], U8)
         nc.vector.quantize_mx(out_codes[:].bitcast(FP8X4), out_scales[:], out_bf[:].rearrange("p q t -> p (q t)"))

@@ -24,6 +24,9 @@ ROWS = QUADRANTS * LIVE
 RUN = 4
 SPARE = 4
 
+SHARED = (2, 3)
+CUT = I // 2
+
 KB = 1024
 SCALES_AT = 0
 KN_AT = 4 * KB
@@ -32,7 +35,7 @@ RAW_AT = 32 * KB
 QN_AT = RAW_AT + 4 * KB
 QUERY_AT = 40 * KB
 COEF_AT = [52 * KB, WORDS_AT + 2 * KB, KN_AT + 4 * KB, QUERY_AT + KB]
-PICKED_AT = [QN_AT - 3 * KB // 4, COEF_AT[0], RAW_AT + KB + KB // 2, 60 * KB]
+PICKED_AT = [QN_AT - 3 * KB // 4, COEF_AT[0], RAW_AT + KB + KB // 2, RAW_AT + KB]
 LATE_AT = COEF_AT[3] + 2 * KB
 
 
@@ -143,7 +146,11 @@ def tile_attend_kernelridge_pl_kernel(tc, query, pts_words, pts_scales, kn, qn, 
 
         def gather(t):
             picked[t] = placed(f"picked{t}", [P, I], BF16, PICKED_AT[t])
-            nc.vector.tensor_copy(picked[t][:], coef_all[t][:].indirect(offsets[:]))
+            if t in SHARED:
+                nc.vector.tensor_copy(picked[t][:, :CUT], coef_all[t][:].indirect(offsets[:, : CUT // 16]))
+                nc.scalar.activation(picked[t][:, CUT:], coef_all[t][:].indirect(offsets[:, CUT // 16 :]), ACT.Copy)
+            else:
+                nc.vector.tensor_copy(picked[t][:], coef_all[t][:].indirect(offsets[:]))
 
         def turn(t):
             pairs = picked[t][:].bitcast(F32)

@@ -244,15 +244,18 @@ def tile_attend_kernelridge_pl_kernel(tc, query, pts_words, pts_scales, kn, qn, 
         late = [ps.tile([P, 2, P], F32, name=f"late{h}", tag=f"turn{h}") for h in range(HALVES)]
         for h, cols in enumerate(halves):
             product(late[h][:, 0, :], 2, cols)
+        results = [own(f"result{t}", [P, Q], F32) for t in range(2, PACK)]
+        for h, copy in enumerate(copies):
+            copy(results[0][:, halves[h]], late[h][:, 0, :])
+        nc.sync.dma_start(out_planes[:, 2, :], results[0][:])
         quantise(3)
         for h, cols in enumerate(halves):
             product(late[h][:, 1, :], 3, cols)
 
-        result_late = own("result_late", [P, 2, Q], F32)
         for h, copy in enumerate(copies):
             copy(out_bf[:, halves[h], 2:], late[h][:].rearrange("p t q -> p q t"))
-            copy(result_late[:, :, halves[h]], late[h][:])
-        nc.scalar.dma_start(out_planes[:, 2:, :], result_late[:])
+            copy(results[1][:, halves[h]], late[h][:, 1, :])
+        nc.sync.dma_start(out_planes[:, 3, :], results[1][:])
         out_codes = own("out_codes", [P, Q], U32)
         out_scales = own("out_scales", [P, Q], U8)
         nc.vector.quantize_mx(out_codes[:].bitcast(FP8X4), out_scales[:], out_bf[:].rearrange("p q t -> p (q t)"))

@@ -32,10 +32,12 @@ SCALES_AT = 0
 KN_AT = 4 * KB
 WORDS_AT = 18 * KB
 RAW_AT = 32 * KB
-QN_AT = RAW_AT + 4 * KB
+QN_AT = 96 * KB
 QUERY_AT = 40 * KB
-COEF_AT = [52 * KB, WORDS_AT + 2 * KB, KN_AT + 4 * KB, QUERY_AT + KB]
-PICKED_AT = [QN_AT - 3 * KB // 4, COEF_AT[0], RAW_AT + KB + KB // 2, RAW_AT + KB]
+COEF_AT = [52 * KB, WORDS_AT + 2 * KB, QN_AT - 8 * KB + 64, QUERY_AT + KB]
+PICKED_AT = [QUERY_AT, COEF_AT[0], RAW_AT + KB + KB // 2, COEF_AT[2] + 4 * KB]
+V_LAST_AT = 60 * KB
+CODES_AT = [COEF_AT[2] + 3 * KB, COEF_AT[2] + 3 * KB + KB // 2, COEF_AT[3] + 2 * KB]
 LATE_AT = COEF_AT[3] + 2 * KB
 
 
@@ -105,7 +107,6 @@ def tile_attend_kernelridge_pl_kernel(tc, query, pts_words, pts_scales, kn, qn, 
         nc.vector.tensor_copy(
             kn_row[:].bitcast(U32).rearrange("r (t p) -> r p t", t=PACK), kn_all[:].bitcast(U32).indirect(offsets[:])
         )
-        nc.sync.dma_start(coef_all[2][:], coef_planes[:, 2, :])
 
         query_bf = placed("query_bf", [P, Q, PACK], BF16, QUERY_AT)
         for cols in halves:
@@ -116,6 +117,7 @@ def tile_attend_kernelridge_pl_kernel(tc, query, pts_words, pts_scales, kn, qn, 
 
         qn_turned = ps.tile([P, P], F32, name="qn_turned", tag="columns")
         nc.tensor.transpose(qn_turned[:], qn_rows[:], ident[:])
+        nc.sync.dma_start(coef_all[2][:], coef_planes[:, 2, :])
         qn_col = placed("qn_col", [P, HALVES], F32, RAW_AT + 2 * KB + KB // 2)
         nc.scalar.copy(qn_col[:], qn_turned[:, P - HALVES :])
 
@@ -159,13 +161,13 @@ def tile_attend_kernelridge_pl_kernel(tc, query, pts_words, pts_scales, kn, qn, 
                 nc.tensor.transpose(turned[t][:, u, :], pairs[:, u::2], ident[:])
 
         def empty(t):
-            v_bf[t] = own(f"v_bf{t}", [P, P * PACK], BF16)
+            v_bf[t] = placed("v_bf3", [P, P * PACK], BF16, V_LAST_AT) if t == 3 else own(f"v_bf{t}", [P, P * PACK], BF16)
             nc.scalar.copy(
                 v_bf[t][:].bitcast(F32).rearrange("p (m u) -> p m u", u=2), turned[t][:].rearrange("p u m -> p m u")
             )
 
         def quantise(t):
-            v_codes[t] = placed("v_codes2", [P, P], U32, LATE_AT) if t == 2 else own(f"v_codes{t}", [P, P], U32)
+            v_codes[t] = placed(f"v_codes{t}", [P, P], U32, CODES_AT[t]) if t < 3 else own(f"v_codes{t}", [P, P], U32)
             v_scales[t] = own(f"v_scales{t}", [P, P], U8)
             nc.vector.quantize_mx(v_codes[t][:].bitcast(FP8X4), v_scales[t][:], v_bf[t][:])
 
@@ -206,7 +208,7 @@ def tile_attend_kernelridge_pl_kernel(tc, query, pts_words, pts_scales, kn, qn, 
                 mybir.AluOpType.mult,
             )
         gather(2)
-        w_codes = own("w_codes", [P, Q], U32)
+        w_codes = placed("w_codes", [P, Q], U32, COEF_AT[2] + 2 * KB)
         w_scales = own("w_scales", [P, Q], U8)
         for h, cols in enumerate(halves):
             nc.vector.quantize_mx(
@@ -225,37 +227,38 @@ def tile_attend_kernelridge_pl_kernel(tc, query, pts_words, pts_scales, kn, qn, 
             )
 
         out_planes = out_0.rearrange("(p t) q -> p t q", t=PACK)
-        out_bf = placed("out_bf", [P, Q, PACK], BF16, LATE_AT + KB)
-        early = [ps.tile([P, 2, P], F32, name=f"early{h}", tag=f"wide{h}") for h in range(HALVES)]
-        result_early = own("result_early", [P, 2, Q], F32)
+        last = PACK - 1
+        early = [ps.tile([P, last, P], F32, name=f"early{h}", tag=f"wide{h}") for h in range(HALVES)]
+        result_early = placed("result_early", [P, 2, Q], F32, COEF_AT[3] + 4 * KB)
         for t in range(2):
             for h, cols in enumerate(halves):
                 product(early[h][:, t, :], t, cols)
-        for h, cols in enumerate(halves):
-            nc.scalar.copy(result_early[:, :, cols], early[h][:])
+        copies = [nc.vector.tensor_copy, nc.scalar.copy]
+        for h, copy in enumerate(copies):
+            copy(result_early[:, :, halves[h]], early[h][:, :2, :])
         nc.sync.dma_start(out_planes[:, :2, :], result_early[:])
 
-        copies = [nc.vector.tensor_copy, nc.scalar.copy]
         quantise(2)
-        for h in reversed(range(HALVES)):
-            copies[h](out_bf[:, halves[h], :2], early[h][:].rearrange("p t q -> p q t"))
-        turn(3)
-        empty(3)
-        late = [ps.tile([P, 2, P], F32, name=f"late{h}", tag=f"turn{h}") for h in range(HALVES)]
+        turn(last)
+        empty(last)
         for h, cols in enumerate(halves):
-            product(late[h][:, 0, :], 2, cols)
+            product(early[h][:, 2, :], 2, cols)
         results = [own(f"result{t}", [P, Q], F32) for t in range(2, PACK)]
-        for h, copy in enumerate(copies):
-            copy(results[0][:, halves[h]], late[h][:, 0, :])
-        nc.sync.dma_start(out_planes[:, 2, :], results[0][:])
-        quantise(3)
         for h, cols in enumerate(halves):
-            product(late[h][:, 1, :], 3, cols)
-
+            nc.scalar.copy(results[0][:, cols], early[h][:, 2, :])
+        nc.sync.dma_start(out_planes[:, 2, :], results[0][:])
+        quantise(last)
+        out_bf = placed("out_bf", [P, Q, PACK], BF16, V_LAST_AT)
         for h, copy in enumerate(copies):
-            copy(out_bf[:, halves[h], 2:], late[h][:].rearrange("p t q -> p q t"))
-            copy(results[1][:, halves[h]], late[h][:, 1, :])
-        nc.sync.dma_start(out_planes[:, 3, :], results[1][:])
+            copy(out_bf[:, halves[h], :last], early[h][:].rearrange("p t q -> p q t"))
+
+        late = [ps.tile([P, P], F32, name=f"late{h}", tag=f"turn{h}") for h in range(HALVES)]
+        for h, cols in enumerate(halves):
+            product(late[h][:], last, cols)
+        for h, copy in enumerate(copies):
+            copy(out_bf[:, halves[h], last], late[h][:])
+            copy(results[1][:, halves[h]], late[h][:])
+        nc.sync.dma_start(out_planes[:, last, :], results[1][:])
         out_codes = own("out_codes", [P, Q], U32)
         out_scales = own("out_scales", [P, Q], U8)
         nc.vector.quantize_mx(out_codes[:].bitcast(FP8X4), out_scales[:], out_bf[:].rearrange("p q t -> p (q t)"))

@@ -37,6 +37,7 @@ QUERY_AT = 40 * KB
 COEF_AT = [52 * KB, WORDS_AT + 2 * KB, QN_AT - 8 * KB + 64, QUERY_AT + KB]
 PICKED_AT = [QUERY_AT, COEF_AT[0], RAW_AT + KB + KB // 2, COEF_AT[2] + 4 * KB]
 V_LAST_AT = 60 * KB
+V_AT = [62 * KB, COEF_AT[2] + 6 * KB, 63 * KB, V_LAST_AT]
 CODES_AT = [COEF_AT[2] + 3 * KB, COEF_AT[2] + 3 * KB + KB // 2, COEF_AT[3] + 2 * KB]
 LATE_AT = COEF_AT[3] + 2 * KB
 
@@ -57,14 +58,13 @@ def tile_attend_kernelridge_pl_kernel(tc, query, pts_words, pts_scales, kn, qn, 
         halves = [slice(h * P, (h + 1) * P) for h in range(HALVES)]
 
         offsets = sb.tile([P, I // 16], U16, name="offsets")
-        words_all = placed("words_all", [P, T], U16, WORDS_AT)
+        words_all = own("words_all", [P, T], U16)
         scales_all = placed("scales_all", [P, T + SPARE], U8, SCALES_AT)
         kn_all = placed("kn_all", [P, T], F32, KN_AT)
         query_raw = placed("query_raw", [P, PACK, Q], F32, RAW_AT)
         qn_rows = placed("qn_rows", [P, P], F32, QN_AT)
         coef_all = [placed(f"coef_all{t}", [P, T], F32, COEF_AT[t]) for t in range(PACK)]
-        zeros = own("zeros", [P, P], F32)
-        ident = own("ident", [P, P], F32)
+        zeros = placed("zeros", [P, P], F32, COEF_AT[1] - 256)
         scales = own("scales", [P, I + SPARE], U8)
 
         first_row = P // 2 - ROWS
@@ -77,12 +77,8 @@ def tile_attend_kernelridge_pl_kernel(tc, query, pts_words, pts_scales, kn, qn, 
         nc.scalar.dma_start(qn_rows[P - HALVES :, :], qn.rearrange("(h p) o -> h (p o)", p=P))
         nc.sync.dma_start(coef_all[0][:], coef_planes[:, 0, :])
 
-        nc.gpsimd.memset(kn_all[: P - 1, : 3 * T // 4].bitcast(I32), 0)
         nc.gpsimd.memset(zeros[:], 0.0)
-        nc.gpsimd.affine_select(
-            out=ident[:], in_=zeros[:], compare_op=mybir.AluOpType.not_equal, fill=1.0,
-            base=0, pattern=[[-1, P]], channel_multiplier=1,
-        )
+        nc.gpsimd.memset(kn_all[: P - 1, : 3 * T // 4].bitcast(I32), 0)
         nc.scalar.copy(qn_rows[: P - HALVES, :], zeros[: P - HALVES, :])
         nc.vector.memset(scales_all[:first_row, :].bitcast(I32), 0)
         nc.vector.memset(scales_all[P // 2 :, :].bitcast(I32), 0)
@@ -92,16 +88,21 @@ def tile_attend_kernelridge_pl_kernel(tc, query, pts_words, pts_scales, kn, qn, 
         scale_rows = own("scale_rows", [P, I], U8)
         nc.vector.tensor_copy(scale_rows[:], scales_all[:, :T].indirect(offsets[:]))
         for row in range(LIVE):
-            nc.scalar.dma_start(
+            nc.sync.dma_start(
                 scales[row :: P // QUADRANTS, :I].bitcast(I32),
                 scale_rows[first_row + row : P // 2 : LIVE, :].bitcast(I32),
             )
+        ident = placed("ident", [P, P], F32, SCALES_AT + 2 * KB)
+        nc.gpsimd.affine_select(
+            out=ident[:], in_=zeros[:], compare_op=mybir.AluOpType.not_equal, fill=1.0,
+            base=0, pattern=[[-1, P]], channel_multiplier=1,
+        )
+        us_col = placed("us_col", [P, PACK], F32, COEF_AT[1] - 128)
+        nc.sync.dma_start(coef_all[1][:], coef_planes[:, 1, :])
+        nc.sync.dma_start(us_col[:], us.rearrange("o (p t) -> p (o t)", t=PACK))
 
         words = own("words", [P, I], U16)
         nc.vector.tensor_copy(words[:], words_all[:].indirect(offsets[:]))
-        us_col = placed("us_col", [P, PACK], F32, WORDS_AT)
-        nc.sync.dma_start(coef_all[1][:], coef_planes[:, 1, :])
-        nc.sync.dma_start(us_col[:], us.rearrange("o (p t) -> p (o t)", t=PACK))
 
         kn_row = placed("kn_row", [P, I], F32, SCALES_AT)
         nc.vector.tensor_copy(
@@ -161,7 +162,7 @@ def tile_attend_kernelridge_pl_kernel(tc, query, pts_words, pts_scales, kn, qn, 
                 nc.tensor.transpose(turned[t][:, u, :], pairs[:, u::2], ident[:])
 
         def empty(t):
-            v_bf[t] = placed("v_bf3", [P, P * PACK], BF16, V_LAST_AT) if t == 3 else own(f"v_bf{t}", [P, P * PACK], BF16)
+            v_bf[t] = placed(f"v_bf{t}", [P, P * PACK], BF16, V_AT[t])
             nc.scalar.copy(
                 v_bf[t][:].bitcast(F32).rearrange("p (m u) -> p m u", u=2), turned[t][:].rearrange("p u m -> p m u")
             )
@@ -196,7 +197,7 @@ def tile_attend_kernelridge_pl_kernel(tc, query, pts_words, pts_scales, kn, qn, 
         gather(1)
         for t in range(2):
             turn(t)
-            empty(t)
+        empty(0)
 
         w_bf = []
         for h in range(HALVES):
@@ -208,6 +209,7 @@ def tile_attend_kernelridge_pl_kernel(tc, query, pts_words, pts_scales, kn, qn, 
                 mybir.AluOpType.mult,
             )
         gather(2)
+        empty(1)
         w_codes = placed("w_codes", [P, Q], U32, COEF_AT[2] + 2 * KB)
         w_scales = own("w_scales", [P, Q], U8)
         for h, cols in enumerate(halves):

@@ -37,7 +37,7 @@ QUERY_AT = 40 * KB
 COEF_AT = [52 * KB, WORDS_AT + 2 * KB, QN_AT - 8 * KB + 64, QUERY_AT + KB]
 PICKED_AT = [QUERY_AT, COEF_AT[0], RAW_AT + KB + KB // 2, COEF_AT[2] + 4 * KB]
 V_LAST_AT = 60 * KB
-V_AT = [62 * KB, COEF_AT[2] + 6 * KB, 63 * KB, V_LAST_AT]
+V_AT = [62 * KB, COEF_AT[2] + 6 * KB, COEF_AT[3] + 6 * KB, V_LAST_AT]
 CODES_AT = [COEF_AT[2] + 3 * KB, COEF_AT[2] + 3 * KB + KB // 2, COEF_AT[3] + 2 * KB]
 LATE_AT = COEF_AT[3] + 2 * KB
 
@@ -219,8 +219,8 @@ def tile_attend_kernelridge_pl_kernel(tc, query, pts_words, pts_scales, kn, qn, 
         quantise(0)
         quantise(1)
         turn(2)
-        empty(2)
         gather(3)
+        empty(2)
 
         def product(out, t, cols):
             nc.tensor.matmul_mx(
@@ -246,24 +246,27 @@ def tile_attend_kernelridge_pl_kernel(tc, query, pts_words, pts_scales, kn, qn, 
         for h, cols in enumerate(halves):
             product(early[h][:, 2, :], 2, cols)
         results = [own(f"result{t}", [P, Q], F32) for t in range(2, PACK)]
-        for h, cols in enumerate(halves):
-            nc.scalar.copy(results[0][:, cols], early[h][:, 2, :])
+        out_bf = [placed("out_bf0", [P, P, PACK], BF16, V_LAST_AT), own("out_bf1", [P, P, PACK], BF16)]
+        nc.scalar.copy(results[0][:, halves[0]], early[0][:, 2, :])
+        nc.scalar.copy(out_bf[1][:, :, :last], early[1][:].rearrange("p t q -> p q t"))
+        nc.scalar.copy(results[0][:, halves[1]], early[1][:, 2, :])
         nc.sync.dma_start(out_planes[:, 2, :], results[0][:])
         quantise(last)
-        out_bf = placed("out_bf", [P, Q, PACK], BF16, V_LAST_AT)
-        for h, copy in enumerate(copies):
-            copy(out_bf[:, halves[h], :last], early[h][:].rearrange("p t q -> p q t"))
+        nc.vector.tensor_copy(out_bf[0][:, :, :last], early[0][:].rearrange("p t q -> p q t"))
 
         late = [ps.tile([P, P], F32, name=f"late{h}", tag=f"turn{h}") for h in range(HALVES)]
         for h, cols in enumerate(halves):
             product(late[h][:], last, cols)
         for h, copy in enumerate(copies):
-            copy(out_bf[:, halves[h], last], late[h][:])
+            copy(out_bf[h][:, :, last], late[h][:])
             copy(results[1][:, halves[h]], late[h][:])
         nc.sync.dma_start(out_planes[:, last, :], results[1][:])
         out_codes = own("out_codes", [P, Q], U32)
         out_scales = own("out_scales", [P, Q], U8)
-        nc.vector.quantize_mx(out_codes[:].bitcast(FP8X4), out_scales[:], out_bf[:].rearrange("p q t -> p (q t)"))
+        for h, cols in enumerate(halves):
+            nc.vector.quantize_mx(
+                out_codes[:, cols].bitcast(FP8X4), out_scales[:, cols], out_bf[h][:].rearrange("p q t -> p (q t)")
+            )
         nc.sync.dma_start(out_1[0].rearrange("p q r -> p (q r)").bitcast(I32), out_codes[:].bitcast(I32))
         for quad in range(QUADRANTS):
             queue = nc.sync if quad % 2 else nc.scalar

@@ -22,7 +22,7 @@ QUADRANTS = 4
 LIVE = 4
 ROWS = QUADRANTS * LIVE
 RUN = 4
-SPARE = 4
+ODD_CUT = T // 2 - 4
 
 SHARED = (2, 3)
 CUT = I // 2
@@ -39,7 +39,6 @@ PICKED_AT = [QUERY_AT, COEF_AT[0], RAW_AT + KB + KB // 2, COEF_AT[2] + 4 * KB]
 V_LAST_AT = 60 * KB
 V_AT = [62 * KB, COEF_AT[2] + 6 * KB, COEF_AT[3] + 6 * KB, V_LAST_AT]
 CODES_AT = [COEF_AT[2] + 3 * KB, COEF_AT[2] + 3 * KB + KB // 2, COEF_AT[3] + 2 * KB]
-LATE_AT = COEF_AT[3] + 2 * KB
 
 
 def tile_attend_kernelridge_pl_kernel(tc, query, pts_words, pts_scales, kn, qn, us, coef, offs, out_0, out_1, out_2):
@@ -59,18 +58,18 @@ def tile_attend_kernelridge_pl_kernel(tc, query, pts_words, pts_scales, kn, qn, 
 
         offsets = sb.tile([P, I // 16], U16, name="offsets")
         words_all = own("words_all", [P, T], U16)
-        scales_all = placed("scales_all", [P, T + SPARE], U8, SCALES_AT)
+        scales_all = placed("scales_all", [P, T], U8, SCALES_AT)
         kn_all = placed("kn_all", [P, T], F32, KN_AT)
         query_raw = placed("query_raw", [P, PACK, Q], F32, RAW_AT)
         qn_rows = placed("qn_rows", [P, P], F32, QN_AT)
         coef_all = [placed(f"coef_all{t}", [P, T], F32, COEF_AT[t]) for t in range(PACK)]
         zeros = placed("zeros", [P, P], F32, COEF_AT[1] - 256)
-        scales = own("scales", [P, I + SPARE], U8)
+        scales = own("scales", [P, I], U8)
 
         first_row = P // 2 - ROWS
         coef_planes = coef.rearrange("(p t) n -> p t n", t=PACK)
         nc.sync.dma_start(offsets[:], offs)
-        nc.scalar.dma_start(scales_all[first_row : P // 2, :T].bitcast(I32), pts_scales[0].bitcast(I32))
+        nc.scalar.dma_start(scales_all[first_row : P // 2, :].bitcast(I32), pts_scales[0].bitcast(I32))
         nc.scalar.dma_start(kn_all[P - 1 :, :], kn[0:1, :])
         nc.sync.dma_start(words_all[:].bitcast(I32), pts_words[0].bitcast(I32))
         nc.sync.dma_start(query_raw[:], query.rearrange("(p j) q -> p j q", j=PACK))
@@ -80,19 +79,20 @@ def tile_attend_kernelridge_pl_kernel(tc, query, pts_words, pts_scales, kn, qn, 
         nc.gpsimd.memset(zeros[:], 0.0)
         nc.gpsimd.memset(kn_all[: P - 1, : 3 * T // 4].bitcast(I32), 0)
         nc.scalar.copy(qn_rows[: P - HALVES, :], zeros[: P - HALVES, :])
-        nc.vector.memset(scales_all[:first_row, :].bitcast(I32), 0)
-        nc.vector.memset(scales_all[P // 2 :, :].bitcast(I32), 0)
+        for rows in (slice(0, first_row), slice(P // 2, P)):
+            for cols in (slice(0, ODD_CUT), slice(ODD_CUT, T)):
+                nc.vector.memset(scales_all[rows, cols].bitcast(I32), 0)
         nc.vector.memset(scales[:].bitcast(I32), 0)
         nc.vector.memset(kn_all[: P - 1, 3 * T // 4 :].bitcast(I32), 0)
 
         scale_rows = own("scale_rows", [P, I], U8)
-        nc.vector.tensor_copy(scale_rows[:], scales_all[:, :T].indirect(offsets[:]))
+        nc.vector.tensor_copy(scale_rows[:], scales_all[:].indirect(offsets[:]))
         for row in range(LIVE):
             nc.sync.dma_start(
-                scales[row :: P // QUADRANTS, :I].bitcast(I32),
+                scales[row :: P // QUADRANTS, :].bitcast(I32),
                 scale_rows[first_row + row : P // 2 : LIVE, :].bitcast(I32),
             )
-        ident = placed("ident", [P, P], F32, SCALES_AT + 2 * KB)
+        ident = placed("ident", [P, P], F32, SCALES_AT)
         nc.gpsimd.affine_select(
             out=ident[:], in_=zeros[:], compare_op=mybir.AluOpType.not_equal, fill=1.0,
             base=0, pattern=[[-1, P]], channel_multiplier=1,
@@ -104,7 +104,7 @@ def tile_attend_kernelridge_pl_kernel(tc, query, pts_words, pts_scales, kn, qn, 
         words = own("words", [P, I], U16)
         nc.vector.tensor_copy(words[:], words_all[:].indirect(offsets[:]))
 
-        kn_row = placed("kn_row", [P, I], F32, SCALES_AT)
+        kn_row = placed("kn_row", [P, I], F32, SCALES_AT + KB // 2)
         nc.vector.tensor_copy(
             kn_row[:].bitcast(U32).rearrange("r (t p) -> r p t", t=PACK), kn_all[:].bitcast(U32).indirect(offsets[:])
         )
@@ -142,7 +142,7 @@ def tile_attend_kernelridge_pl_kernel(tc, query, pts_words, pts_scales, kn, qn, 
             dots.append(ps.tile([P, I], F32, name=f"dots{h}", tag=f"wide{h}"))
             nc.tensor.matmul_mx(
                 dots[h][:], lhsT=query_codes[:, cols].bitcast(FP8X4), lhsT_scale=query_scales[:, cols],
-                rhs=words[:].bitcast(FP4X4), rhs_scale=scales[:, :I], start=True, stop=True,
+                rhs=words[:].bitcast(FP4X4), rhs_scale=scales[:], start=True, stop=True,
             )
 
         picked, turned, v_bf, v_codes, v_scales = {}, {}, {}, {}, {}

@@ -269,7 +269,7 @@ def tile_attend_kernelridge_pl_kernel(tc, query, pts_words, pts_scales, kn, qn, 
             )
         nc.sync.dma_start(out_1[0].rearrange("p q r -> p (q r)").bitcast(I32), out_codes[:].bitcast(I32))
         for quad in range(QUADRANTS):
-            queue = nc.sync if quad % 2 else nc.scalar
+            queue = nc.sync if quad == QUADRANTS - 1 else nc.scalar
             first = quad * (P // QUADRANTS)
             queue.dma_start(
                 out_2[0, LIVE * quad : LIVE * (quad + 1), :].bitcast(I32),

@@ -257,9 +257,10 @@ def tile_attend_kernelridge_pl_kernel(tc, query, pts_words, pts_scales, kn, qn, 
         late = [ps.tile([P, P], F32, name=f"late{h}", tag=f"turn{h}") for h in range(HALVES)]
         for h, cols in enumerate(halves):
             product(late[h][:], last, cols)
-        for h, copy in enumerate(copies):
-            copy(out_bf[h][:, :, last], late[h][:])
-            copy(results[1][:, halves[h]], late[h][:])
+        nc.vector.tensor_copy(out_bf[0][:, :, last], late[0][:])
+        nc.vector.tensor_copy(results[1][:, halves[0]], late[0][:])
+        nc.scalar.copy(results[1][:, halves[1]], late[1][:])
+        nc.scalar.copy(out_bf[1][:, :, last], late[1][:])
         nc.sync.dma_start(out_planes[:, last, :], results[1][:])
         out_codes = own("out_codes", [P, Q], U32)
         out_scales = own("out_scales", [P, Q], U8)

@@ -231,6 +231,7 @@ def tile_attend_kernelridge_pl_kernel(tc, query, pts_words, pts_scales, kn, qn, 
         out_planes = out_0.rearrange("(p t) q -> p t q", t=PACK)
         last = PACK - 1
         early = [ps.tile([P, last, P], F32, name=f"early{h}", tag=f"wide{h}") for h in range(HALVES)]
+        late = [ps.tile([P, 2 - h, P], F32, name=f"late{h}", tag=f"turn{h}") for h in range(HALVES)]
         result_early = placed("result_early", [P, 2, Q], F32, COEF_AT[3] + 4 * KB)
         for t in range(2):
             for h, cols in enumerate(halves):
@@ -241,26 +242,26 @@ def tile_attend_kernelridge_pl_kernel(tc, query, pts_words, pts_scales, kn, qn, 
         nc.sync.dma_start(out_planes[:, :2, :], result_early[:])
 
         quantise(2)
+        out_bf = [placed("out_bf0", [P, P, PACK], BF16, COEF_AT[3] + 7 * KB), own("out_bf1", [P, P, PACK], BF16)]
+        nc.vector.tensor_copy(out_bf[0][:, :, :2], early[0][:, :2, :].rearrange("p t q -> p q t"))
         turn(last)
         empty(last)
         for h, cols in enumerate(halves):
             product(early[h][:, 2, :], 2, cols)
+        product(late[0][:, 0, :], 2, halves[0])
         results = [own(f"result{t}", [P, Q], F32) for t in range(2, PACK)]
-        out_bf = [placed("out_bf0", [P, P, PACK], BF16, V_LAST_AT), own("out_bf1", [P, P, PACK], BF16)]
         nc.scalar.copy(results[0][:, halves[0]], early[0][:, 2, :])
         nc.scalar.copy(out_bf[1][:, :, :last], early[1][:].rearrange("p t q -> p q t"))
         nc.scalar.copy(results[0][:, halves[1]], early[1][:, 2, :])
         nc.sync.dma_start(out_planes[:, 2, :], results[0][:])
         quantise(last)
-        nc.vector.tensor_copy(out_bf[0][:, :, :last], early[0][:].rearrange("p t q -> p q t"))
 
-        late = [ps.tile([P, P], F32, name=f"late{h}", tag=f"turn{h}") for h in range(HALVES)]
         for h, cols in enumerate(halves):
-            product(late[h][:], last, cols)
-        nc.vector.tensor_copy(out_bf[0][:, :, last], late[0][:])
-        nc.vector.tensor_copy(results[1][:, halves[0]], late[0][:])
-        nc.scalar.copy(results[1][:, halves[1]], late[1][:])
-        nc.scalar.copy(out_bf[1][:, :, last], late[1][:])
+            product(late[h][:, 1 - h, :], last, cols)
+        nc.vector.tensor_copy(out_bf[0][:, :, 2:], late[0][:].rearrange("p t q -> p q t"))
+        nc.vector.tensor_copy(results[1][:, halves[0]], late[0][:, 1, :])
+        nc.scalar.copy(results[1][:, halves[1]], late[1][:, 0, :])
+        nc.scalar.copy(out_bf[1][:, :, last], late[1][:, 0, :])
         nc.sync.dma_start(out_planes[:, last, :], results[1][:])
         out_codes = own("out_codes", [P, Q], U32)
         out_scales = own("out_scales", [P, Q], U8)

@@ -230,38 +230,37 @@ def tile_attend_kernelridge_pl_kernel(tc, query, pts_words, pts_scales, kn, qn, 
 
         out_planes = out_0.rearrange("(p t) q -> p t q", t=PACK)
         last = PACK - 1
-        early = [ps.tile([P, last, P], F32, name=f"early{h}", tag=f"wide{h}") for h in range(HALVES)]
-        late = [ps.tile([P, 2 - h, P], F32, name=f"late{h}", tag=f"turn{h}") for h in range(HALVES)]
+        early = [ps.tile([P, 2, P], F32, name=f"early{h}", tag=f"wide{h}") for h in range(HALVES)]
+        late = [ps.tile([P, 2, P], F32, name=f"late{h}", tag=f"turn{h}") for h in range(HALVES)]
         result_early = placed("result_early", [P, 2, Q], F32, COEF_AT[3] + 4 * KB)
+        out_bf = [placed(f"out_bf{h}", [P, P, PACK], BF16, COEF_AT[3] + (7 - 4 * h) * KB) for h in range(HALVES)]
         for t in range(2):
             for h, cols in enumerate(halves):
                 product(early[h][:, t, :], t, cols)
         copies = [nc.vector.tensor_copy, nc.scalar.copy]
         for h, copy in enumerate(copies):
-            copy(result_early[:, :, halves[h]], early[h][:, :2, :])
+            copy(result_early[:, :, halves[h]], early[h][:])
         nc.sync.dma_start(out_planes[:, :2, :], result_early[:])
 
         quantise(2)
-        out_bf = [placed("out_bf0", [P, P, PACK], BF16, COEF_AT[3] + 7 * KB), own("out_bf1", [P, P, PACK], BF16)]
-        nc.vector.tensor_copy(out_bf[0][:, :, :2], early[0][:, :2, :].rearrange("p t q -> p q t"))
+        nc.vector.tensor_copy(out_bf[0][:, :, :2], early[0][:].rearrange("p t q -> p q t"))
         turn(last)
         empty(last)
+        nc.scalar.copy(out_bf[1][:, :, :2], early[1][:].rearrange("p t q -> p q t"))
+        plane2 = ps.tile([P, Q], F32, name="plane2", tag="columns")
+        product(plane2[:], 2, slice(0, Q))
         for h, cols in enumerate(halves):
-            product(early[h][:, 2, :], 2, cols)
-        product(late[0][:, 0, :], 2, halves[0])
-        results = [own(f"result{t}", [P, Q], F32) for t in range(2, PACK)]
-        nc.scalar.copy(results[0][:, halves[0]], early[0][:, 2, :])
-        nc.scalar.copy(out_bf[1][:, :, :last], early[1][:].rearrange("p t q -> p q t"))
-        nc.scalar.copy(results[0][:, halves[1]], early[1][:, 2, :])
-        nc.sync.dma_start(out_planes[:, 2, :], results[0][:])
+            product(late[h][:, 0, :], 2, cols)
+        results = [placed("result2", [P, Q], F32, V_LAST_AT), own("result3", [P, Q], F32)]
         quantise(last)
+        nc.vector.tensor_copy(results[0][:], plane2[:])
+        nc.sync.dma_start(out_planes[:, 2, :], results[0][:])
 
         for h, cols in enumerate(halves):
-            product(late[h][:, 1 - h, :], last, cols)
-        nc.vector.tensor_copy(out_bf[0][:, :, 2:], late[0][:].rearrange("p t q -> p q t"))
-        nc.vector.tensor_copy(results[1][:, halves[0]], late[0][:, 1, :])
-        nc.scalar.copy(results[1][:, halves[1]], late[1][:, 0, :])
-        nc.scalar.copy(out_bf[1][:, :, last], late[1][:, 0, :])
+            product(late[h][:, 1, :], last, cols)
+        for h, copy in enumerate(copies):
+            copy(out_bf[h][:, :, 2:], late[h][:].rearrange("p t q -> p q t"))
+            copy(results[1][:, halves[h]], late[h][:, 1, :])
         nc.sync.dma_start(out_planes[:, last, :], results[1][:])
         out_codes = own("out_codes", [P, Q], U32)
         out_scales = own("out_scales", [P, Q], U8)

from contextlib import ExitStack

import concourse.mybir as mybir

D, T, I, Q, E = 512, 2048, 512, 256, 512
FLOPS = 2 * D * Q * I + 2 * I * E * Q

F32 = mybir.dt.float32
BF16 = mybir.dt.bfloat16
I32 = mybir.dt.int32
U32 = mybir.dt.uint32
U16 = mybir.dt.uint16
U8 = mybir.dt.uint8
FP8X4 = mybir.dt.float8_e4m3fn_x4
FP4X4 = mybir.dt.float4_e2m1fn_x4
ACT = mybir.ActivationFunctionType

P = 128
PACK = 4
HALVES = Q // P
QUADRANTS = 4
LIVE = 4
ROWS = QUADRANTS * LIVE
RUN = 4
ODD_CUT = T // 2 - 4

SHARED = (2, 3)
CUT = I // 2

KB = 1024
SCALES_AT = 0
KN_AT = 4 * KB
WORDS_AT = 18 * KB
RAW_AT = 32 * KB
QN_AT = 96 * KB
QUERY_AT = 40 * KB
COEF_AT = [52 * KB, WORDS_AT + 2 * KB, QN_AT - 8 * KB + 64, QUERY_AT + KB]
PICKED_AT = [QUERY_AT, COEF_AT[0], RAW_AT + KB + KB // 2, COEF_AT[2] + 4 * KB]
V_LAST_AT = 60 * KB
V_AT = [62 * KB, COEF_AT[2] + 6 * KB, COEF_AT[3] + 6 * KB, V_LAST_AT]
CODES_AT = [COEF_AT[2] + 3 * KB, COEF_AT[2] + 3 * KB + KB // 2, COEF_AT[3] + 2 * KB]


def tile_attend_kernelridge_pl_kernel(tc, query, pts_words, pts_scales, kn, qn, us, coef, offs, out_0, out_1, out_2):
    nc = tc.nc
    with ExitStack() as ctx:
        sb = ctx.enter_context(tc.tile_pool(name="sb", bufs=1))
        shared = ctx.enter_context(tc.tile_pool(name="shared", bufs=1))
        ps = ctx.enter_context(tc.psum_pool(name="ps", bufs=1))

        def placed(name, shape, dtype, offset):
            return shared.tile(shape, dtype, name=name, align_bytes=64, offset=offset)

        def own(name, shape, dtype):
            return sb.tile(shape, dtype, name=name, align_bytes=64)

        halves = [slice(h * P, (h + 1) * P) for h in range(HALVES)]

        offsets = sb.tile([P, I // 16], U16, name="offsets")
        words_all = own("words_all", [P, T], U16)
        scales_all = placed("scales_all", [P, T], U8, SCALES_AT)
        kn_all = placed("kn_all", [P, T], F32, KN_AT)
        query_raw = placed("query_raw", [P, PACK, Q], F32, RAW_AT)
        qn_rows = placed("qn_rows", [P, P], F32, QN_AT)
        coef_all = [placed(f"coef_all{t}", [P, T], F32, COEF_AT[t]) for t in range(PACK)]
        zeros = placed("zeros", [P, P], F32, COEF_AT[1] - 256)
        scales = own("scales", [P, I], U8)

        first_row = P // 2 - ROWS
        coef_planes = coef.rearrange("(p t) n -> p t n", t=PACK)
        nc.sync.dma_start(offsets[:], offs)
        nc.scalar.dma_start(scales_all[first_row : P // 2, :].bitcast(I32), pts_scales[0].bitcast(I32))
        nc.scalar.dma_start(kn_all[P - 1 :, :], kn[0:1, :])
        nc.sync.dma_start(words_all[:].bitcast(I32), pts_words[0].bitcast(I32))
        nc.sync.dma_start(query_raw[:], query.rearrange("(p j) q -> p j q", j=PACK))
        nc.scalar.dma_start(qn_rows[P - HALVES :, :], qn.rearrange("(h p) o -> h (p o)", p=P))
        nc.sync.dma_start(coef_all[0][:], coef_planes[:, 0, :])

        nc.gpsimd.memset(zeros[:], 0.0)
        nc.gpsimd.memset(kn_all[: P - 1, : 3 * T // 4].bitcast(I32), 0)
        nc.scalar.copy(qn_rows[: P - HALVES, :], zeros[: P - HALVES, :])
        for rows in (slice(0, first_row), slice(P // 2, P)):
            for cols in (slice(0, ODD_CUT), slice(ODD_CUT, T)):
                nc.vector.memset(scales_all[rows, cols].bitcast(I32), 0)
        nc.vector.memset(scales[:].bitcast(I32), 0)
        nc.vector.memset(kn_all[: P - 1, 3 * T // 4 :].bitcast(I32), 0)

        scale_rows = own("scale_rows", [P, I], U8)
        nc.vector.tensor_copy(scale_rows[:], scales_all[:].indirect(offsets[:]))
        for row in range(LIVE):
            nc.sync.dma_start(
                scales[row :: P // QUADRANTS, :].bitcast(I32),
                scale_rows[first_row + row : P // 2 : LIVE, :].bitcast(I32),
            )
        ident = placed("ident", [P, P], F32, SCALES_AT)
        nc.gpsimd.affine_select(
            out=ident[:], in_=zeros[:], compare_op=mybir.AluOpType.not_equal, fill=1.0,
            base=0, pattern=[[-1, P]], channel_multiplier=1,
        )
        us_col = placed("us_col", [P, PACK], F32, COEF_AT[1] - 128)
        nc.sync.dma_start(coef_all[1][:], coef_planes[:, 1, :])
        nc.sync.dma_start(us_col[:], us.rearrange("o (p t) -> p (o t)", t=PACK))

        words = own("words", [P, I], U16)
        nc.vector.tensor_copy(words[:], words_all[:].indirect(offsets[:]))

        kn_row = placed("kn_row", [P, I], F32, SCALES_AT + KB // 2)
        nc.vector.tensor_copy(
            kn_row[:].bitcast(U32).rearrange("r (t p) -> r p t", t=PACK), kn_all[:].bitcast(U32).indirect(offsets[:])
        )

        query_bf = placed("query_bf", [P, Q, PACK], BF16, QUERY_AT)
        for cols in halves:
            nc.scalar.copy(
                query_bf[:, cols, :].rearrange("p (c i) j -> p c j i", i=RUN),
                query_raw[:, :, cols].rearrange("p j (c i) -> p c j i", i=RUN),
            )

        qn_turned = ps.tile([P, P], F32, name="qn_turned", tag="columns")
        nc.tensor.transpose(qn_turned[:], qn_rows[:], ident[:])
        nc.sync.dma_start(coef_all[2][:], coef_planes[:, 2, :])
        qn_col = placed("qn_col", [P, HALVES], F32, RAW_AT + 2 * KB + KB // 2)
        nc.scalar.copy(qn_col[:], qn_turned[:, P - HALVES :])

        kn_turned = ps.tile([P, PACK, P], F32, name="kn_turned", tag="columns")
        neg_kn = placed("neg_kn", [P, PACK], F32, RAW_AT + 2 * KB)
        for t in range(PACK):
            nc.tensor.transpose(kn_turned[:, t, :], kn_row[:, t * P : (t + 1) * P], ident[:])
        nc.scalar.activation(neg_kn[:], kn_turned[:, :, P - 1], ACT.Copy, scale=-1.0)

        query_codes = placed("query_codes", [P, Q], U32, KN_AT + 2 * KB)
        query_scales = placed("query_scales", [P, Q], U8, QN_AT + KB // 4)
        for cols in halves:
            nc.vector.quantize_mx(
                query_codes[:, cols].bitcast(FP8X4), query_scales[:, cols],
                query_bf[:, cols, :].rearrange("p q j -> p (q j)"),
            )
        nc.sync.dma_start(coef_all[3][:], coef_planes[:, 3, :])

        dots = []
        for h, cols in enumerate(halves):
            dots.append(ps.tile([P, I], F32, name=f"dots{h}", tag=f"wide{h}"))
            nc.tensor.matmul_mx(
                dots[h][:], lhsT=query_codes[:, cols].bitcast(FP8X4), lhsT_scale=query_scales[:, cols],
                rhs=words[:].bitcast(FP4X4), rhs_scale=scales[:], start=True, stop=True,
            )

        picked, turned, v_bf, v_codes, v_scales = {}, {}, {}, {}, {}

        def gather(t):
            picked[t] = placed(f"picked{t}", [P, I], BF16, PICKED_AT[t])
            if t in SHARED:
                nc.vector.tensor_copy(picked[t][:, :CUT], coef_all[t][:].indirect(offsets[:, : CUT // 16]))
                nc.scalar.activation(picked[t][:, CUT:], coef_all[t][:].indirect(offsets[:, CUT // 16 :]), ACT.Copy)
            else:
                nc.vector.tensor_copy(picked[t][:], coef_all[t][:].indirect(offsets[:]))

        def turn(t):
            pairs = picked[t][:].bitcast(F32)
            turned[t] = ps.tile([P, 2, P], F32, name=f"turned{t}", tag=f"turn{t}")
            for u in range(2):
                nc.tensor.transpose(turned[t][:, u, :], pairs[:, u::2], ident[:])

        def empty(t):
            v_bf[t] = placed(f"v_bf{t}", [P, P * PACK], BF16, V_AT[t])
            nc.scalar.copy(
                v_bf[t][:].bitcast(F32).rearrange("p (m u) -> p m u", u=2), turned[t][:].rearrange("p u m -> p m u")
            )

        def quantise(t):
            v_codes[t] = placed(f"v_codes{t}", [P, P], U32, CODES_AT[t]) if t < 3 else own(f"v_codes{t}", [P, P], U32)
            v_scales[t] = own(f"v_scales{t}", [P, P], U8)
            nc.vector.quantize_mx(v_codes[t][:].bitcast(FP8X4), v_scales[t][:], v_bf[t][:])

        gather(0)

        gap = []
        for h in range(HALVES):
            gap.append(own(f"gap{h}", [P, PACK, P], F32))
            nc.scalar.activation(
                gap[h][:].rearrange("q t (c i) -> q c t i", i=RUN),
                dots[h][:].rearrange("q (c i t) -> q c t i", i=RUN, t=PACK),
                ACT.Identity, bias=qn_col[:, h : h + 1], scale=-1.0,
            )

        kern = []
        for h in range(HALVES):
            gap_turned = ps.tile([P, PACK, P], F32, name=f"gap_turned{h}", tag=f"turn{h}")
            for t in range(PACK):
                nc.tensor.transpose(gap_turned[:, t, :], gap[h][:, t, :], ident[:])
            kern.append(own(f"kern{h}", [P, PACK, P], F32))
            for t in range(PACK):
                nc.scalar.activation(
                    kern[h][:, t, :], gap_turned[:, t, :], ACT.Exp, bias=neg_kn[:, t : t + 1], scale=-1.0
                )

        gather(1)
        for t in range(2):
            turn(t)
        empty(0)

        w_bf = []
        for h in range(HALVES):
            w_bf.append(own(f"w_bf{h}", [P, P, PACK], BF16))
            nc.vector.tensor_tensor(
                w_bf[h][:].rearrange("p (c i) t -> p c t i", i=RUN),
                kern[h][:].rearrange("p t (c i) -> p c t i", i=RUN),
                us_col[:].unsqueeze(1).unsqueeze(3).to_broadcast([P, P // RUN, PACK, RUN]),
                mybir.AluOpType.mult,
            )
        gather(2)
        empty(1)
        w_codes = placed("w_codes", [P, Q], U32, COEF_AT[2] + 2 * KB)
        w_scales = own("w_scales", [P, Q], U8)
        for h, cols in enumerate(halves):
            nc.vector.quantize_mx(
                w_codes[:, cols].bitcast(FP8X4), w_scales[:, cols], w_bf[h][:].rearrange("p q t -> p (q t)")
            )
        quantise(0)
        quantise(1)
        turn(2)
        gather(3)
        empty(2)

        def product(out, t, cols):
            nc.tensor.matmul_mx(
                out, lhsT=v_codes[t][:].bitcast(FP8X4), lhsT_scale=v_scales[t][:],
                rhs=w_codes[:, cols].bitcast(FP8X4), rhs_scale=w_scales[:, cols], start=True, stop=True,
            )

        out_planes = out_0.rearrange("(p t) q -> p t q", t=PACK)
        last = PACK - 1
        early = [ps.tile([P, 2, P], F32, name=f"early{h}", tag=f"wide{h}") for h in range(HALVES)]
        late = [ps.tile([P, 2, P], F32, name=f"late{h}", tag=f"turn{h}") for h in range(HALVES)]
        result_early = placed("result_early", [P, 2, Q], F32, COEF_AT[3] + 4 * KB)
        out_bf = [placed(f"out_bf{h}", [P, P, PACK], BF16, COEF_AT[3] + (7 - 4 * h) * KB) for h in range(HALVES)]
        for t in range(2):
            for h, cols in enumerate(halves):
                product(early[h][:, t, :], t, cols)
        copies = [nc.vector.tensor_copy, nc.scalar.copy]
        for h, copy in enumerate(copies):
            copy(result_early[:, :, halves[h]], early[h][:])
        nc.sync.dma_start(out_planes[:, :2, :], result_early[:])

        quantise(2)
        nc.vector.tensor_copy(out_bf[0][:, :, :2], early[0][:].rearrange("p t q -> p q t"))
        turn(last)
        empty(last)
        nc.scalar.copy(out_bf[1][:, :, :2], early[1][:].rearrange("p t q -> p q t"))
        plane2 = ps.tile([P, Q], F32, name="plane2", tag="columns")
        product(plane2[:], 2, slice(0, Q))
        for h, cols in enumerate(halves):
            product(late[h][:, 0, :], 2, cols)
        results = [placed("result2", [P, Q], F32, V_LAST_AT), own("result3", [P, Q], F32)]
        quantise(last)
        nc.vector.tensor_copy(results[0][:], plane2[:])
        nc.sync.dma_start(out_planes[:, 2, :], results[0][:])

        for h, cols in enumerate(halves):
            product(late[h][:, 1, :], last, cols)
        for h, copy in enumerate(copies):
            copy(out_bf[h][:, :, 2:], late[h][:].rearrange("p t q -> p q t"))
            copy(results[1][:, halves[h]], late[h][:, 1, :])
        nc.sync.dma_start(out_planes[:, last, :], results[1][:])
        out_codes = own("out_codes", [P, Q], U32)
        out_scales = own("out_scales", [P, Q], U8)
        for h, cols in enumerate(halves):
            nc.vector.quantize_mx(
                out_codes[:, cols].bitcast(FP8X4), out_scales[:, cols], out_bf[h][:].rearrange("p q t -> p (q t)")
            )
        nc.sync.dma_start(out_1[0].rearrange("p q r -> p (q r)").bitcast(I32), out_codes[:].bitcast(I32))
        for quad in range(QUADRANTS):
            queue = nc.sync if quad == QUADRANTS - 1 else nc.scalar
            first = quad * (P // QUADRANTS)
            queue.dma_start(
                out_2[0, LIVE * quad : LIVE * (quad + 1), :].bitcast(I32),
                out_scales[first : first + LIVE, :].bitcast(I32),
            )
